import numpy as np
import ml_dtypes


def mxq(x, axis, fmt="e4m3"):
    dtype, down = {"e4m3": (ml_dtypes.float8_e4m3fn, 7), "e5m2": (ml_dtypes.float8_e5m2, 14)}[fmt]
    v = np.moveaxis(np.asarray(x, np.float32).astype(ml_dtypes.bfloat16).astype(np.float64), axis, -1)
    blocks = v.reshape(v.shape[:-1] + (-1, 32))
    amax = np.abs(blocks).max(-1, keepdims=True)
    byte = np.maximum(np.where(amax > 0, np.frexp(amax)[1] - 1 + 127, 0) - down, 1)
    scale = np.exp2(byte - 127.0)
    codes = (blocks / scale).astype(np.float32).astype(dtype).astype(np.float64)
    return np.moveaxis((codes * scale).reshape(v.shape), -1, axis)


WIDE = False


def mx_kscale(k):
    if not WIDE:
        return np.ones(k)
    levels = np.array([10, -10, 5, -5, 0])
    if k % 512:
        return np.exp2(np.random.permutation(np.resize(levels, k // 32))).repeat(32)
    a = np.empty((k // 512, 16))
    for p in range(k // 512):
        a[p, :8] = np.random.permutation(np.resize(levels, 8))
        for g in range(8):
            far = levels[np.abs(levels - a[p, g]) >= 10]
            a[p, g + 8] = far[np.random.randint(len(far))]
    return np.exp2(a.ravel()).repeat(32)


def f64(x):
    return np.asarray(x).astype(np.float64)


def striped(idx):
    return np.tile(idx.reshape(-1, 16).T, (8, 1)).astype(np.uint16)


def unstriped(offs):
    return offs[:16].T.reshape(-1).astype(np.int64)


E2M1 = np.array([0.0, 0.5, 1.0, 1.5, 2.0, 3.0, 4.0, 6.0, -0.0, -0.5, -1.0, -1.5, -2.0, -3.0, -4.0, -6.0])


def pack_weight(w, fmt):
    k, n = w.shape
    w = f64(np.asarray(w, np.float32).astype(ml_dtypes.bfloat16)).reshape(k // 32, 32, n)
    amax = np.abs(w).max(1)
    if fmt == "e4m3":
        byte = np.frexp(amax)[1] - 1 + 127 - 7
    else:
        mant, ex = np.frexp(amax / 6.0)
        byte = np.where(mant > 0.5, ex, ex - 1) + 127
    byte = np.clip(np.where(amax > 0, byte, 1), 1, 254)
    scaled = (w * np.exp2(127.0 - byte)[:, None, :]).reshape(k, n).astype(np.float32)
    by_word = np.ascontiguousarray(scaled.reshape(k // 512, 128, 4, n).transpose(0, 1, 3, 2))
    if fmt == "e4m3":
        words = by_word.astype(ml_dtypes.float8_e4m3fn).view(np.uint8)
    else:
        c = by_word.astype(ml_dtypes.float4_e2m1fn).view(np.uint8) & 0xF
        words = (c[..., 0::2] | (c[..., 1::2] << 4)).reshape(k // 512, 128, 2 * n)
    return np.ascontiguousarray(words), np.ascontiguousarray(byte.astype(np.uint8).reshape(k // 512, 16, n))


def unpack_weight(words, scales, fmt):
    g, _, n = scales.shape
    words = np.ascontiguousarray(words).reshape(g, 128, n, -1)
    if fmt == "e4m3":
        vals = words.view(ml_dtypes.float8_e4m3fn).astype(np.float64)
    else:
        nib = np.empty((g, 128, n, 4), np.uint8)
        nib[..., 0::2] = words & 0xF
        nib[..., 1::2] = words >> 4
        vals = E2M1[nib]
    vals = vals * np.repeat(np.exp2(scales.astype(np.float64) - 127.0), 8, axis=1)[..., None]
    return vals.transpose(0, 1, 3, 2).reshape(g * 512, n)


def gelu(v):
    return 0.5 * v * (1.0 + np.tanh(np.sqrt(2.0 / np.pi) * (v + 0.044715 * v**3)))


K1, K2, K3, H, N, T1, T2, T3, S = 1024, 1024, 512, 1024, 512, 2048, 1024, 2048, 512

def setup_inputs():
    n = np.random.standard_normal
    s1 = mx_kscale(K1)[:, None]
    s2 = mx_kscale(K2)[:, None]
    s3 = mx_kscale(K3)[:, None]
    u = mx_kscale(H)[:, None]
    tab_words, tab_scales = pack_weight(n((K1, T1)) * s1, "e4m3")
    tab2_words, tab2_scales = pack_weight(n((K2, T2)) * s2, "e4m3")
    tab3_words, tab3_scales = pack_weight(n((K3, T3)) * s3, "e2m1")
    w1_words, w1_scales = pack_weight(n((K1, H)) / np.sqrt(K1) / s1, "e2m1")
    w3_words, w3_scales = pack_weight(n((K3, H)) / np.sqrt(K3) / s3, "e4m3")
    return {
        "tab_words": tab_words, "tab_scales": tab_scales,
        "tab2_words": tab2_words, "tab2_scales": tab2_scales,
        "tab3_words": tab3_words, "tab3_scales": tab3_scales,
        "offs": striped(np.random.permutation(T1)[:S]),
        "offs2": striped(np.random.permutation(T2)[:S]),
        "offs3": striped(np.random.permutation(T3)[:S]),
        "w1_words": w1_words, "w1_scales": w1_scales,
        "w2": (n((K2, H)) / np.sqrt(K2) / s2).astype(np.float32),
        "w3_words": w3_words, "w3_scales": w3_scales,
        "gain": (np.exp(0.3 * n(H)) * u[:, 0]).astype(np.float32),
        "wo": (n((H, N)) / np.sqrt(H) / u).astype(np.float32),
    }

def reference(tab_words, tab_scales, tab2_words, tab2_scales, tab3_words, tab3_scales, offs, offs2, offs3,
              w1_words, w1_scales, w2, w3_words, w3_scales, gain, wo):
    v = unpack_weight(tab_words, tab_scales, "e4m3")[:, unstriped(offs)]
    v2 = unpack_weight(tab2_words, tab2_scales, "e4m3")[:, unstriped(offs2)]
    v3 = unpack_weight(tab3_words, tab3_scales, "e2m1")[:, unstriped(offs3)]
    w1 = unpack_weight(w1_words, w1_scales, "e2m1")
    w3 = unpack_weight(w3_words, w3_scales, "e4m3")
    seed = w1.T @ v
    soil = mxq(f64(w2), 0, "e4m3").T @ v2
    rain = w3.T @ v3
    both = (1.0 / (1.0 + np.exp(-seed))) * (1.0 / (1.0 + np.exp(-soil)))
    h = f64(gain)[:, None] * (np.log(both) + rain)
    out = mxq(f64(wo), 0, "e4m3").T @ mxq(h, 0, "e4m3")
    return out

@@ -1,0 +1,262 @@
+from contextlib import ExitStack
+
+import concourse.mybir as mybir
+from concourse.masks import make_identity
+
+K1, K2, K3, H, N, T1, T2, T3, S = 1024, 1024, 512, 1024, 512, 2048, 1024, 2048, 512
+FLOPS = 2 * S * (K1 * H + K2 * H + K3 * H + H * N)
+
+F32 = mybir.dt.float32
+BF16 = mybir.dt.bfloat16
+I32 = mybir.dt.int32
+U32 = mybir.dt.uint32
+U16 = mybir.dt.uint16
+U8 = mybir.dt.uint8
+FP8X4 = mybir.dt.float8_e4m3fn_x4
+FP4X4 = mybir.dt.float4_e2m1fn_x4
+ACT = mybir.ActivationFunctionType
+ALU = mybir.AluOpType
+
+P = 128
+JC = 128
+NC = S // JC
+TAB2_ROW = 8
+W2_CAST_ON_VECTOR = (4, 2, 4, 3)
+
+
+def tile_list_seed_bank_germination_kernel(
+    tc, tab_words, tab_scales, tab2_words, tab2_scales, tab3_words, tab3_scales, offs, offs2, offs3,
+    w1_words, w1_scales, w2, w3_words, w3_scales, gain, wo, out,
+):
+    nc = tc.nc
+    with ExitStack() as ctx:
+        keep = ctx.enter_context(tc.tile_pool(name="keep", bufs=1))
+        psum = ctx.enter_context(tc.psum_pool(name="psum", bufs=8))
+
+        def sb(name, shape, dtype, tag=None):
+            return keep.tile(shape, dtype, name=name, tag=tag or name, align_bytes=64)
+
+        def bank(name):
+            return psum.tile([P, 4, JC], F32, name=name, tag="bank")
+
+        list1 = keep.tile([P, S // 16], U16, name="list1")
+        list2 = keep.tile([P, S // 16], U16, name="list2")
+        list3 = keep.tile([P, S // 16], U16, name="list3")
+
+        tab_w = [sb("tab_w%d" % a, [P, T1], I32) for a in range(2)]
+        tab_s = sb("tab_s", [P, T1], U8)
+        tab2_w = sb("tab2_w", [P, 2 * T2], I32)
+        tab2_s = sb("tab2_s", [P, T2], U8)
+        tab3_w = sb("tab3_w", [P, T3], U16)
+        tab3_s = sb("tab3_s", [P, T3], U8)
+        w1_raw = sb("w1_raw", [P, 4 * H], U8)
+        w3_raw = sb("w3_raw", [P, H], I32)
+        w13s_raw = sb("w13s_raw", [P, 3 * H], U8)
+        v1_plane = sb("v1_plane", [P, 2 * S], U8)
+        v3_plane = sb("v3_plane", [P, S], U8)
+        gain_rows = sb("gain_rows", [P, P], F32)
+        ident = sb("ident", [P, P], F32)
+        warm = sb("warm", [P, 1], F32)
+        warm_out = sb("warm_out", [P, 1], F32)
+
+        nc.vector.memset(tab_s[:].bitcast(I32), 0)
+        nc.vector.memset(w13s_raw[:].bitcast(I32), 0)
+        nc.vector.memset(tab2_s[:].bitcast(I32), 0)
+        nc.vector.memset(tab3_s[:].bitcast(I32), 0)
+        nc.gpsimd.memset(warm[:], 0.0)
+        nc.gpsimd.memset(v1_plane[:].bitcast(I32), 0)
+        nc.gpsimd.memset(v3_plane[:].bitcast(I32), 0)
+        nc.gpsimd.memset(gain_rows[:], 0.0)
+        make_identity(nc, ident[:])
+        nc.scalar.activation(warm_out[:], warm[:], ACT.Sigmoid)
+
+        w2_raw = [sb("w2_raw%d" % i, [P, 4, 512], F32) for i in range(4)]
+        wo_raw = [sb("wo_raw%d" % b, [P, 4, N], F32) for b in range(2)]
+
+        def load_w2(i):
+            b, a = divmod(i, 2)
+            nc.sync.dma_start(out=w2_raw[i][:], in_=w2[512 * a : 512 * (a + 1), 512 * b : 512 * (b + 1)].rearrange("(p j) c -> p j c", j=4))
+
+        def load_tab(a):
+            nc.sync.dma_start(out=tab_w[a][:], in_=tab_words[a].rearrange("p t i -> p (t i)").bitcast(I32))
+
+        nc.sync.dma_start(list1[:], offs)
+        nc.sync.dma_start(out=tab_s[0:P:4, :].bitcast(I32), in_=tab_scales.rearrange("a q t -> q a t").bitcast(I32))
+        load_tab(0)
+        nc.sync.dma_start(out=w1_raw[:].rearrange("p (a c) -> p a c", a=2).bitcast(I32), in_=w1_words.rearrange("a p c -> p a c").bitcast(I32))
+        for q in range(4):
+            nc.sync.dma_start(
+                out=w13s_raw[32 * q : 32 * q + 4, 0 : 2 * H].rearrange("p (a c) -> p a c", a=2).bitcast(I32),
+                in_=w1_scales[:, 4 * q : 4 * q + 4, :].rearrange("a r c -> r a c").bitcast(I32))
+        load_tab(1)
+        v1_rows = sb("v1_rows", [P, S], U8)
+        nc.vector.tensor_copy(v1_rows[:], tab_s[:].indirect(list1[:]))
+        for q in range(4):
+            nc.sync.dma_start(
+                out=v1_plane[32 * q : 32 * q + 4, :].rearrange("p (a j) -> p a j", a=2).bitcast(I32),
+                in_=v1_rows[32 * q : 32 * q + 32 : 4, :].bitcast(I32))
+        load_w2(0)
+        nc.sync.dma_start(list2[:], offs2)
+        nc.sync.dma_start(out=tab2_w[:].rearrange("p (a t) -> p a t", a=2), in_=tab2_words.rearrange("a p t i -> p a (t i)").bitcast(I32))
+        for q in range(4):
+            nc.sync.dma_start(out=tab2_s[32 * q + TAB2_ROW : 32 * q + TAB2_ROW + 8, :].bitcast(I32), in_=tab2_scales[:, 4 * q : 4 * q + 4, :].bitcast(I32))
+        load_w2(1)
+        nc.sync.dma_start(list3[:], offs3)
+        nc.sync.dma_start(out=tab3_s[0:P:8, :].bitcast(I32), in_=tab3_scales[0].bitcast(I32))
+        load_w2(2)
+        for q in range(4):
+            nc.sync.dma_start(out=w13s_raw[32 * q : 32 * q + 4, 2 * H : 3 * H].bitcast(I32), in_=w3_scales[0, 4 * q : 4 * q + 4, :].bitcast(I32))
+        load_w2(3)
+        v3_rows = sb("v3_rows", [P, S], U8)
+        nc.vector.tensor_copy(v3_rows[:], tab3_s[:].indirect(list3[:]))
+        for q in range(4):
+            nc.sync.dma_start(out=v3_plane[32 * q : 32 * q + 4, :].bitcast(I32), in_=v3_rows[32 * q : 32 * q + 32 : 8, :].bitcast(I32))
+        nc.sync.dma_start(out=tab3_w[:].bitcast(I32), in_=tab3_words[0].bitcast(I32))
+        nc.sync.dma_start(out=w3_raw[:], in_=w3_words[0].rearrange("p c i -> p (c i)").bitcast(I32))
+        for b in range(2):
+            nc.sync.dma_start(
+                out=gain_rows[4 * b : 4 * b + 4, :].rearrange("t (g i) -> t g i", i=8),
+                in_=gain[512 * b : 512 * (b + 1)].rearrange("(g t i) -> t g i", t=4, i=8))
+        for b in range(2):
+            rows = wo[512 * b : 512 * (b + 1), :].rearrange("(g t i) n -> t g i n", t=4, i=8)
+            for t in range(4):
+                nc.sync.dma_start(out=wo_raw[b][:, t, :], in_=rows[t])
+
+        v1 = [sb("v1_%d" % a, [P, S], U32) for a in range(2)]
+        nc.vector.tensor_copy(v1[0][:], tab_w[0][:].bitcast(U32).indirect(list1[:]))
+        w1_p = sb("w1_p", [P, 4 * H], U8)
+        nc.vector.tensor_copy(
+            w1_p[:].bitcast(I32).rearrange("p (x t g w) -> p x t g w", t=4, g=16, w=4),
+            w1_raw[:].bitcast(I32).rearrange("p (x g t w) -> p x t g w", t=4, g=16, w=4))
+        w13s = sb("w13s", [P, 3 * H], U8)
+        nc.vector.tensor_copy(
+            w13s[:, 0 : 2 * H].bitcast(I32).rearrange("p (x t g w) -> p x t g w", t=4, g=16, w=2),
+            w13s_raw[:, 0 : 2 * H].bitcast(I32).rearrange("p (x g t w) -> p x t g w", t=4, g=16, w=2))
+        nc.vector.tensor_copy(v1[1][:], tab_w[1][:].bitcast(U32).indirect(list1[:]))
+
+        sig_seed = sb("sig_seed", [P, 2, NC, 512], F32)
+        for b in range(2):
+            for c in range(NC):
+                acc = bank("seed")
+                for a in range(2):
+                    for t in range(4):
+                        col = a * H + b * 512 + t * P
+                        nc.tensor.matmul_mx(
+                            out=acc[:, t, :],
+                            lhsT=w1_p[:, 2 * col : 2 * (col + P)].bitcast(FP4X4), lhsT_scale=w13s[:, col : col + P],
+                            rhs=v1[a][:, c * JC : (c + 1) * JC].bitcast(FP8X4), rhs_scale=v1_plane[:, a * S + c * JC : a * S + (c + 1) * JC],
+                            start=(a == 0 and t == 0), stop=(a == 1 and t == 3))
+                nc.scalar.activation(sig_seed[:, b, c, :].rearrange("p (j t) -> p j t", t=4), acc[:].rearrange("p t j -> p j t"), ACT.Sigmoid)
+
+        w2_bf = [sb("w2_bf%d" % i, [P, 4, 512], BF16) for i in range(4)]
+        w2_q = [sb("w2_q%d" % i, [P, 512], U32) for i in range(4)]
+        w2_s = [sb("w2_s%d" % i, [P, 512], U8) for i in range(4)]
+
+        def quantize_w2(i):
+            src = w2_raw[i][:].rearrange("p j (g t u w) -> p t g u j w", t=4, u=2, w=4)
+            for t in range(4):
+                dst = w2_bf[i][:, t, :].rearrange("p (g u w j) -> p g u j w", u=2, w=4, j=4)
+                if t < W2_CAST_ON_VECTOR[i]:
+                    nc.vector.tensor_copy(dst, src[:, t])
+                else:
+                    nc.scalar.copy(dst, src[:, t])
+            nc.vector.quantize_mx(out=w2_q[i][:].bitcast(FP8X4), scales=w2_s[i][:], in_=w2_bf[i][:].rearrange("p t x -> p (t x)"))
+
+        quantize_w2(0)
+        v2 = [sb("v2_%d" % a, [P, S], U32) for a in range(2)]
+        v2_plane = sb("v2_plane", [P, S], U8)
+        nc.vector.tensor_copy(v2[0][:], tab2_w[:, 0:T2].bitcast(U32).indirect(list2[:]))
+        nc.vector.tensor_copy(v2_plane[:], tab2_s[:].indirect(list2[:]))
+        nc.vector.tensor_copy(v2[1][:], tab2_w[:, T2 : 2 * T2].bitcast(U32).indirect(list2[:]))
+
+        both = sb("both", [P, NC, 2, 512], F32)
+        gain_pt = sb("gain_pt", [P, 8], F32)
+        sig_soil = sb("sig_soil", [P, 2, NC, 512], F32)
+        for b in range(2):
+            if b == 1:
+                quantize_w2(2)
+            quantize_w2(2 * b + 1)
+            accs = [bank("soil") for c in range(NC)]
+            for a in range(2):
+                i = 2 * b + a
+                row = TAB2_ROW + 4 * a
+                for c in range(NC):
+                    for t in range(4):
+                        nc.tensor.matmul_mx(
+                            out=accs[c][:, t, :],
+                            lhsT=w2_q[i][:, t * P : (t + 1) * P].bitcast(FP8X4), lhsT_scale=w2_s[i][:, t * P : (t + 1) * P],
+                            rhs=v2[a][:, c * JC : (c + 1) * JC].bitcast(FP8X4), rhs_scale=v2_plane[row:P, c * JC : (c + 1) * JC],
+                            start=(a == 0 and t == 0), stop=(a == 1 and t == 3))
+            for c in range(NC):
+                nc.scalar.activation(sig_soil[:, b, c, :].rearrange("p (j t) -> p j t", t=4), accs[c][:].rearrange("p t j -> p j t"), ACT.Sigmoid)
+            for c in range(NC):
+                nc.vector.tensor_tensor(both[:, c, b, :], sig_seed[:, b, c, :], sig_soil[:, b, c, :], ALU.mult)
+
+        gain_bank = bank("gain")
+        nc.tensor.transpose(gain_bank[:, 0, :], gain_rows[:], ident[:])
+        nc.vector.tensor_copy(gain_pt[:], gain_bank[:, 0, 0:8])
+
+        v3 = sb("v3", [P, S], U16)
+        nc.vector.tensor_copy(v3[:], tab3_w[:].indirect(list3[:]))
+        w3_p = sb("w3_p", [P, H], I32)
+        nc.vector.tensor_copy(
+            w3_p[:].rearrange("p (x t g w) -> p x t g w", t=4, g=16, w=8),
+            w3_raw[:].rearrange("p (x g t w) -> p x t g w", t=4, g=16, w=8))
+        nc.vector.tensor_copy(
+            w13s[:, 2 * H : 3 * H].bitcast(I32).rearrange("p (x t g w) -> p x t g w", t=4, g=16, w=2),
+            w13s_raw[:, 2 * H : 3 * H].bitcast(I32).rearrange("p (x g t w) -> p x t g w", t=4, g=16, w=2))
+        rain = {}
+        for c in range(NC):
+            for b in range(2):
+                rain[c, b] = bank("rain")
+                for t in range(4):
+                    col = b * 512 + t * P
+                    nc.tensor.matmul_mx(
+                        out=rain[c, b][:, t, :],
+                        lhsT=w3_p[:, col : col + P].bitcast(FP8X4), lhsT_scale=w13s[:, 2 * H + col : 2 * H + col + P],
+                        rhs=v3[:, c * JC : (c + 1) * JC].bitcast(FP4X4), rhs_scale=v3_plane[:, c * JC : (c + 1) * JC],
+                        start=True, stop=True)
+
+        logs = sb("logs", [P, 2, NC, 512], F32, tag="sig_soil")
+        order = [(c, b) for c in range(NC) for b in range(2)]
+        for c, b in order:
+            nc.scalar.activation(logs[:, b, c, :], both[:, c, b, :], ACT.Ln)
+
+        wo_bf = [sb("wo_bf%d" % b, [P, 4 * N], BF16) for b in range(2)]
+        wo_q = [sb("wo_q%d" % b, [P, N], U32) for b in range(2)]
+        wo_s = [sb("wo_s%d" % b, [P, N], U8) for b in range(2)]
+        for b in range(2):
+            nc.scalar.copy(
+                wo_bf[b][:].rearrange("p (x w t) -> p x t w", w=4, t=4),
+                wo_raw[b][:].rearrange("p t (x w) -> p x t w", w=4))
+
+        summed = sb("summed", [P, NC, 2, 512], F32, tag="sig_seed")
+        h_bf = [sb("h_bf%d" % c, [P, 2 * 512], BF16) for c in range(NC)]
+        h_q = [sb("h_q%d" % c, [P, 2 * JC], U32) for c in range(NC)]
+        h_s = [sb("h_s%d" % c, [P, 2 * JC], U8) for c in range(NC)]
+        gain_b = gain_pt[:].rearrange("p (b t) -> p b t", t=4).unsqueeze(2).to_broadcast([P, 2, JC, 4])
+        for c in range(NC):
+            for b in range(2):
+                nc.vector.tensor_tensor(
+                    summed[:, c, b, :].rearrange("p (j t) -> p j t", t=4), rain[c, b][:].rearrange("p t j -> p j t"),
+                    logs[:, b, c, :].rearrange("p (j t) -> p j t", t=4), ALU.add)
+            nc.vector.tensor_tensor(
+                h_bf[c][:].rearrange("p (b j t) -> p b j t", b=2, t=4),
+                summed[:, c].rearrange("p b (j t) -> p b j t", t=4), gain_b, ALU.mult)
+            nc.vector.quantize_mx(out=h_q[c][:].bitcast(FP8X4), scales=h_s[c][:], in_=h_bf[c][:])
+        for b in range(2):
+            nc.vector.quantize_mx(out=wo_q[b][:].bitcast(FP8X4), scales=wo_s[b][:], in_=wo_bf[b][:])
+
+        out_v = out.rearrange("(m p) j -> p m j", p=P)
+        for c in range(NC):
+            acc = bank("score")
+            for m in range(4):
+                for b in range(2):
+                    nc.tensor.matmul_mx(
+                        out=acc[:, m, :],
+                        lhsT=wo_q[b][:, m * P : (m + 1) * P].bitcast(FP8X4), lhsT_scale=wo_s[b][:, m * P : (m + 1) * P],
+                        rhs=h_q[c][:, b * JC : (b + 1) * JC].bitcast(FP8X4), rhs_scale=h_s[c][:, b * JC : (b + 1) * JC],
+                        start=(b == 0), stop=(b == 1))
+            res = sb("res%d" % c, [P, 4, JC], F32, tag="w2_raw%d" % c)
+            nc.scalar.copy(res[:], acc[:])
+            nc.sync.dma_start(out=out_v[:, :, c * JC : (c + 1) * JC], in_=res[:])

@@ -21,7 +21,6 @@ P = 128
 JC = 128
 NC = S // JC
 TAB2_ROW = 8
-W2_CAST_ON_VECTOR = (4, 2, 4, 3)
 
 
 def tile_list_seed_bank_germination_kernel(
@@ -31,13 +30,15 @@ def tile_list_seed_bank_germination_kernel(
     nc = tc.nc
     with ExitStack() as ctx:
         keep = ctx.enter_context(tc.tile_pool(name="keep", bufs=1))
-        psum = ctx.enter_context(tc.psum_pool(name="psum", bufs=8))
+        psum = ctx.enter_context(tc.psum_pool(name="psum", bufs=1))
+        taken = []
 
         def sb(name, shape, dtype, tag=None):
             return keep.tile(shape, dtype, name=name, tag=tag or name, align_bytes=64)
 
         def bank(name):
-            return psum.tile([P, 4, JC], F32, name=name, tag="bank")
+            taken.append(name)
+            return psum.tile([P, 512], F32, name=name, tag="bank%d" % ((len(taken) - 1) % 8))
 
         list1 = keep.tile([P, S // 16], U16, name="list1")
         list2 = keep.tile([P, S // 16], U16, name="list2")
@@ -49,25 +50,24 @@ def tile_list_seed_bank_germination_kernel(
         tab2_s = sb("tab2_s", [P, T2], U8)
         tab3_w = sb("tab3_w", [P, T3], U16)
         tab3_s = sb("tab3_s", [P, T3], U8)
-        w1_raw = sb("w1_raw", [P, 4 * H], U8)
-        w3_raw = sb("w3_raw", [P, H], I32)
-        w13s_raw = sb("w13s_raw", [P, 3 * H], U8)
+        w1_w = sb("w1_w", [P, 4 * H], U8)
+        w1_s = sb("w1_s", [P, 2 * H], U8)
+        w3_w = sb("w3_w", [P, H], I32)
+        w3_s = sb("w3_s", [P, H], U8)
         v1_plane = sb("v1_plane", [P, 2 * S], U8)
         v3_plane = sb("v3_plane", [P, S], U8)
-        gain_rows = sb("gain_rows", [P, P], F32)
+        gain_pt = sb("gain_pt", [P, 2, 4], F32)
         ident = sb("ident", [P, P], F32)
         warm = sb("warm", [P, 1], F32)
         warm_out = sb("warm_out", [P, 1], F32)
 
-        nc.vector.memset(tab_s[:].bitcast(I32), 0)
-        nc.vector.memset(w13s_raw[:].bitcast(I32), 0)
-        nc.vector.memset(tab2_s[:].bitcast(I32), 0)
         nc.vector.memset(tab3_s[:].bitcast(I32), 0)
+        nc.vector.memset(tab_s[:].bitcast(I32), 0)
+        nc.vector.memset(tab2_s[:].bitcast(I32), 0)
+        nc.vector.memset(w1_s[:].bitcast(I32), 0)
         nc.gpsimd.memset(warm[:], 0.0)
+        nc.gpsimd.memset(w3_s[:].bitcast(I32), 0)
         nc.gpsimd.memset(v1_plane[:].bitcast(I32), 0)
-        nc.gpsimd.memset(v3_plane[:].bitcast(I32), 0)
-        nc.gpsimd.memset(gain_rows[:], 0.0)
-        make_identity(nc, ident[:])
         nc.scalar.activation(warm_out[:], warm[:], ACT.Sigmoid)
 
         w2_raw = [sb("w2_raw%d" % i, [P, 4, 512], F32) for i in range(4)]
@@ -80,183 +80,164 @@ def tile_list_seed_bank_germination_kernel(
         def load_tab(a):
             nc.sync.dma_start(out=tab_w[a][:], in_=tab_words[a].rearrange("p t i -> p (t i)").bitcast(I32))
 
+        for q in range(4):
+            nc.gpsimd.dma_start(out=w3_s[32 * q : 32 * q + 4, :].bitcast(I32), in_=w3_scales[0, 4 * q : 4 * q + 4, :].bitcast(I32))
+        for q in range(4):
+            nc.gpsimd.dma_start(
+                out=w1_s[32 * q : 32 * q + 4, :].rearrange("p (a c) -> p a c", a=2).bitcast(I32),
+                in_=w1_scales[:, 4 * q : 4 * q + 4, :].rearrange("a r c -> r a c").bitcast(I32))
+        nc.sync.dma_start(out=tab3_w[:].bitcast(I32), in_=tab3_words[0].bitcast(I32))
+        nc.sync.dma_start(list3[:], offs3)
+        nc.sync.dma_start(out=w3_w[:], in_=w3_words[0].rearrange("p c i -> p (c i)").bitcast(I32))
+        for q in range(4):
+            nc.sync.dma_start(out=tab3_s[32 * q : 32 * q + 4, :].bitcast(I32), in_=tab3_scales[0, 4 * q : 4 * q + 4, :].bitcast(I32))
+        nc.sync.dma_start(out=tab2_w[:].rearrange("p (a t) -> p a t", a=2), in_=tab2_words.rearrange("a p t i -> p a (t i)").bitcast(I32))
+        nc.sync.dma_start(list2[:], offs2)
         nc.sync.dma_start(list1[:], offs)
         nc.sync.dma_start(out=tab_s[0:P:4, :].bitcast(I32), in_=tab_scales.rearrange("a q t -> q a t").bitcast(I32))
-        load_tab(0)
-        nc.sync.dma_start(out=w1_raw[:].rearrange("p (a c) -> p a c", a=2).bitcast(I32), in_=w1_words.rearrange("a p c -> p a c").bitcast(I32))
+        load_w2(0)
         for q in range(4):
-            nc.sync.dma_start(
-                out=w13s_raw[32 * q : 32 * q + 4, 0 : 2 * H].rearrange("p (a c) -> p a c", a=2).bitcast(I32),
-                in_=w1_scales[:, 4 * q : 4 * q + 4, :].rearrange("a r c -> r a c").bitcast(I32))
-        load_tab(1)
+            nc.sync.dma_start(out=tab2_s[32 * q + TAB2_ROW : 32 * q + TAB2_ROW + 8, :].bitcast(I32), in_=tab2_scales[:, 4 * q : 4 * q + 4, :].bitcast(I32))
+        load_w2(1)
+        v3 = sb("v3", [P, S], U16)
+        nc.vector.tensor_copy(v3[:], tab3_w[:].indirect(list3[:]))
+        nc.vector.tensor_copy(v3_plane[:], tab3_s[:].indirect(list3[:]))
+        v2 = [sb("v2_%d" % a, [P, S], U32) for a in range(2)]
+        v2_plane = sb("v2_plane", [P, S], U8)
+        nc.vector.tensor_copy(v2[0][:], tab2_w[:, 0:T2].bitcast(U32).indirect(list2[:]))
+        nc.vector.tensor_copy(v2[1][:], tab2_w[:, T2 : 2 * T2].bitcast(U32).indirect(list2[:]))
         v1_rows = sb("v1_rows", [P, S], U8)
         nc.vector.tensor_copy(v1_rows[:], tab_s[:].indirect(list1[:]))
+        nc.vector.tensor_copy(v2_plane[:], tab2_s[:].indirect(list2[:]))
+        load_tab(0)
+        nc.sync.dma_start(out=w1_w[:].rearrange("p (a c) -> p a c", a=2).bitcast(I32), in_=w1_words.rearrange("a p c -> p a c").bitcast(I32))
+        load_tab(1)
         for q in range(4):
             nc.sync.dma_start(
                 out=v1_plane[32 * q : 32 * q + 4, :].rearrange("p (a j) -> p a j", a=2).bitcast(I32),
                 in_=v1_rows[32 * q : 32 * q + 32 : 4, :].bitcast(I32))
-        load_w2(0)
-        nc.sync.dma_start(list2[:], offs2)
-        nc.sync.dma_start(out=tab2_w[:].rearrange("p (a t) -> p a t", a=2), in_=tab2_words.rearrange("a p t i -> p a (t i)").bitcast(I32))
-        for q in range(4):
-            nc.sync.dma_start(out=tab2_s[32 * q + TAB2_ROW : 32 * q + TAB2_ROW + 8, :].bitcast(I32), in_=tab2_scales[:, 4 * q : 4 * q + 4, :].bitcast(I32))
-        load_w2(1)
-        nc.sync.dma_start(list3[:], offs3)
-        nc.sync.dma_start(out=tab3_s[0:P:8, :].bitcast(I32), in_=tab3_scales[0].bitcast(I32))
         load_w2(2)
-        for q in range(4):
-            nc.sync.dma_start(out=w13s_raw[32 * q : 32 * q + 4, 2 * H : 3 * H].bitcast(I32), in_=w3_scales[0, 4 * q : 4 * q + 4, :].bitcast(I32))
+        nc.sync.dma_start(out=gain_pt[:], in_=gain.rearrange("(b p t) -> p b t", b=2, t=4))
         load_w2(3)
-        v3_rows = sb("v3_rows", [P, S], U8)
-        nc.vector.tensor_copy(v3_rows[:], tab3_s[:].indirect(list3[:]))
-        for q in range(4):
-            nc.sync.dma_start(out=v3_plane[32 * q : 32 * q + 4, :].bitcast(I32), in_=v3_rows[32 * q : 32 * q + 32 : 8, :].bitcast(I32))
-        nc.sync.dma_start(out=tab3_w[:].bitcast(I32), in_=tab3_words[0].bitcast(I32))
-        nc.sync.dma_start(out=w3_raw[:], in_=w3_words[0].rearrange("p c i -> p (c i)").bitcast(I32))
         for b in range(2):
-            nc.sync.dma_start(
-                out=gain_rows[4 * b : 4 * b + 4, :].rearrange("t (g i) -> t g i", i=8),
-                in_=gain[512 * b : 512 * (b + 1)].rearrange("(g t i) -> t g i", t=4, i=8))
-        for b in range(2):
-            rows = wo[512 * b : 512 * (b + 1), :].rearrange("(g t i) n -> t g i n", t=4, i=8)
-            for t in range(4):
-                nc.sync.dma_start(out=wo_raw[b][:, t, :], in_=rows[t])
+            nc.sync.dma_start(out=wo_raw[b][:], in_=wo[512 * b : 512 * (b + 1), :].rearrange("(p t) n -> p t n", t=4))
 
-        v1 = [sb("v1_%d" % a, [P, S], U32) for a in range(2)]
-        nc.vector.tensor_copy(v1[0][:], tab_w[0][:].bitcast(U32).indirect(list1[:]))
-        w1_p = sb("w1_p", [P, 4 * H], U8)
-        nc.vector.tensor_copy(
-            w1_p[:].bitcast(I32).rearrange("p (x t g w) -> p x t g w", t=4, g=16, w=4),
-            w1_raw[:].bitcast(I32).rearrange("p (x g t w) -> p x t g w", t=4, g=16, w=4))
-        w13s = sb("w13s", [P, 3 * H], U8)
-        nc.vector.tensor_copy(
-            w13s[:, 0 : 2 * H].bitcast(I32).rearrange("p (x t g w) -> p x t g w", t=4, g=16, w=2),
-            w13s_raw[:, 0 : 2 * H].bitcast(I32).rearrange("p (x g t w) -> p x t g w", t=4, g=16, w=2))
-        nc.vector.tensor_copy(v1[1][:], tab_w[1][:].bitcast(U32).indirect(list1[:]))
+        make_identity(nc, ident[:])
 
-        sig_seed = sb("sig_seed", [P, 2, NC, 512], F32)
-        for b in range(2):
-            for c in range(NC):
-                acc = bank("seed")
-                for a in range(2):
-                    for t in range(4):
-                        col = a * H + b * 512 + t * P
-                        nc.tensor.matmul_mx(
-                            out=acc[:, t, :],
-                            lhsT=w1_p[:, 2 * col : 2 * (col + P)].bitcast(FP4X4), lhsT_scale=w13s[:, col : col + P],
-                            rhs=v1[a][:, c * JC : (c + 1) * JC].bitcast(FP8X4), rhs_scale=v1_plane[:, a * S + c * JC : a * S + (c + 1) * JC],
-                            start=(a == 0 and t == 0), stop=(a == 1 and t == 3))
-                nc.scalar.activation(sig_seed[:, b, c, :].rearrange("p (j t) -> p j t", t=4), acc[:].rearrange("p t j -> p j t"), ACT.Sigmoid)
+        def quantize_weight(name, raw, on_vector):
+            grouped = sb(name + "_bf", [P, 4 * 512], BF16)
+            codes = sb(name + "_q", [P, 512], U32)
+            scales = sb(name + "_s", [P, 512], U8)
+            dst = grouped[:].rearrange("p (x w t) -> p x t w", w=4, t=4)
+            src = raw[:].rearrange("p t (x w) -> p x t w", w=4)
+            if on_vector:
+                nc.vector.tensor_copy(dst, src)
+            else:
+                nc.scalar.copy(dst, src)
+            nc.vector.quantize_mx(out=codes[:].bitcast(FP8X4), scales=scales[:], in_=grouped[:])
+            return codes, scales
 
-        w2_bf = [sb("w2_bf%d" % i, [P, 4, 512], BF16) for i in range(4)]
-        w2_q = [sb("w2_q%d" % i, [P, 512], U32) for i in range(4)]
-        w2_s = [sb("w2_s%d" % i, [P, 512], U8) for i in range(4)]
+        def by_t(ap):
+            return ap.rearrange("j (t p) -> j t p", t=4)
 
-        def quantize_w2(i):
-            src = w2_raw[i][:].rearrange("p j (g t u w) -> p t g u j w", t=4, u=2, w=4)
-            for t in range(4):
-                dst = w2_bf[i][:, t, :].rearrange("p (g u w j) -> p g u j w", u=2, w=4, j=4)
-                if t < W2_CAST_ON_VECTOR[i]:
-                    nc.vector.tensor_copy(dst, src[:, t])
-                else:
-                    nc.scalar.copy(dst, src[:, t])
-            nc.vector.quantize_mx(out=w2_q[i][:].bitcast(FP8X4), scales=w2_s[i][:], in_=w2_bf[i][:].rearrange("p t x -> p (t x)"))
+        def from_bank(acc):
+            return acc[:].rearrange("j (p t) -> j t p", t=4)
 
-        quantize_w2(0)
-        v2 = [sb("v2_%d" % a, [P, S], U32) for a in range(2)]
-        v2_plane = sb("v2_plane", [P, S], U8)
-        nc.vector.tensor_copy(v2[0][:], tab2_w[:, 0:T2].bitcast(U32).indirect(list2[:]))
-        nc.vector.tensor_copy(v2_plane[:], tab2_s[:].indirect(list2[:]))
-        nc.vector.tensor_copy(v2[1][:], tab2_w[:, T2 : 2 * T2].bitcast(U32).indirect(list2[:]))
-
-        both = sb("both", [P, NC, 2, 512], F32)
-        gain_pt = sb("gain_pt", [P, 8], F32)
         sig_soil = sb("sig_soil", [P, 2, NC, 512], F32)
-        for b in range(2):
-            if b == 1:
-                quantize_w2(2)
-            quantize_w2(2 * b + 1)
-            accs = [bank("soil") for c in range(NC)]
+        sig_seed = sb("sig_seed", [P, 2, NC, 512], F32)
+        rain = sb("rain", [P, NC, 2, 512], F32)
+
+        def soil(b, pieces, width):
+            parts = [(c, r0) for c in range(NC) for r0 in range(0, 512, width)]
+            accs = [bank("soil") for part in parts]
             for a in range(2):
-                i = 2 * b + a
+                codes, scales = pieces[a]
                 row = TAB2_ROW + 4 * a
-                for c in range(NC):
-                    for t in range(4):
-                        nc.tensor.matmul_mx(
-                            out=accs[c][:, t, :],
-                            lhsT=w2_q[i][:, t * P : (t + 1) * P].bitcast(FP8X4), lhsT_scale=w2_s[i][:, t * P : (t + 1) * P],
-                            rhs=v2[a][:, c * JC : (c + 1) * JC].bitcast(FP8X4), rhs_scale=v2_plane[row:P, c * JC : (c + 1) * JC],
-                            start=(a == 0 and t == 0), stop=(a == 1 and t == 3))
-            for c in range(NC):
-                nc.scalar.activation(sig_soil[:, b, c, :].rearrange("p (j t) -> p j t", t=4), accs[c][:].rearrange("p t j -> p j t"), ACT.Sigmoid)
-            for c in range(NC):
-                nc.vector.tensor_tensor(both[:, c, b, :], sig_seed[:, b, c, :], sig_soil[:, b, c, :], ALU.mult)
-
-        gain_bank = bank("gain")
-        nc.tensor.transpose(gain_bank[:, 0, :], gain_rows[:], ident[:])
-        nc.vector.tensor_copy(gain_pt[:], gain_bank[:, 0, 0:8])
-
-        v3 = sb("v3", [P, S], U16)
-        nc.vector.tensor_copy(v3[:], tab3_w[:].indirect(list3[:]))
-        w3_p = sb("w3_p", [P, H], I32)
-        nc.vector.tensor_copy(
-            w3_p[:].rearrange("p (x t g w) -> p x t g w", t=4, g=16, w=8),
-            w3_raw[:].rearrange("p (x g t w) -> p x t g w", t=4, g=16, w=8))
-        nc.vector.tensor_copy(
-            w13s[:, 2 * H : 3 * H].bitcast(I32).rearrange("p (x t g w) -> p x t g w", t=4, g=16, w=2),
-            w13s_raw[:, 2 * H : 3 * H].bitcast(I32).rearrange("p (x g t w) -> p x t g w", t=4, g=16, w=2))
-        rain = {}
-        for c in range(NC):
-            for b in range(2):
-                rain[c, b] = bank("rain")
-                for t in range(4):
-                    col = b * 512 + t * P
+                for acc, (c, r0) in zip(accs, parts):
                     nc.tensor.matmul_mx(
-                        out=rain[c, b][:, t, :],
-                        lhsT=w3_p[:, col : col + P].bitcast(FP8X4), lhsT_scale=w13s[:, 2 * H + col : 2 * H + col + P],
-                        rhs=v3[:, c * JC : (c + 1) * JC].bitcast(FP4X4), rhs_scale=v3_plane[:, c * JC : (c + 1) * JC],
-                        start=True, stop=True)
+                        out=acc[:, 0:width],
+                        lhsT=v2[a][:, c * JC : (c + 1) * JC].bitcast(FP8X4), lhsT_scale=v2_plane[row:P, c * JC : (c + 1) * JC],
+                        rhs=codes[:, r0 : r0 + width].bitcast(FP8X4), rhs_scale=scales[:, r0 : r0 + width], start=(a == 0), stop=(a == 1))
+            for acc, (c, r0) in zip(accs, parts):
+                nc.scalar.activation(
+                    by_t(sig_soil[:, b, c, :])[:, :, r0 // 4 : (r0 + width) // 4],
+                    acc[:, 0:width].rearrange("j (p t) -> j t p", t=4), ACT.Sigmoid)
 
-        logs = sb("logs", [P, 2, NC, 512], F32, tag="sig_soil")
-        order = [(c, b) for c in range(NC) for b in range(2)]
-        for c, b in order:
-            nc.scalar.activation(logs[:, b, c, :], both[:, c, b, :], ACT.Ln)
-
-        wo_bf = [sb("wo_bf%d" % b, [P, 4 * N], BF16) for b in range(2)]
-        wo_q = [sb("wo_q%d" % b, [P, N], U32) for b in range(2)]
-        wo_s = [sb("wo_s%d" % b, [P, N], U8) for b in range(2)]
-        for b in range(2):
-            nc.scalar.copy(
-                wo_bf[b][:].rearrange("p (x w t) -> p x t w", w=4, t=4),
-                wo_raw[b][:].rearrange("p t (x w) -> p x t w", w=4))
-
-        summed = sb("summed", [P, NC, 2, 512], F32, tag="sig_seed")
-        h_bf = [sb("h_bf%d" % c, [P, 2 * 512], BF16) for c in range(NC)]
-        h_q = [sb("h_q%d" % c, [P, 2 * JC], U32) for c in range(NC)]
-        h_s = [sb("h_s%d" % c, [P, 2 * JC], U8) for c in range(NC)]
-        gain_b = gain_pt[:].rearrange("p (b t) -> p b t", t=4).unsqueeze(2).to_broadcast([P, 2, JC, 4])
         for c in range(NC):
             for b in range(2):
-                nc.vector.tensor_tensor(
-                    summed[:, c, b, :].rearrange("p (j t) -> p j t", t=4), rain[c, b][:].rearrange("p t j -> p j t"),
-                    logs[:, b, c, :].rearrange("p (j t) -> p j t", t=4), ALU.add)
-            nc.vector.tensor_tensor(
-                h_bf[c][:].rearrange("p (b j t) -> p b j t", b=2, t=4),
-                summed[:, c].rearrange("p b (j t) -> p b j t", t=4), gain_b, ALU.mult)
-            nc.vector.quantize_mx(out=h_q[c][:].bitcast(FP8X4), scales=h_s[c][:], in_=h_bf[c][:])
+                acc = bank("rain")
+                nc.tensor.matmul_mx(
+                    out=acc[:],
+                    lhsT=v3[:, c * JC : (c + 1) * JC].bitcast(FP4X4), lhsT_scale=v3_plane[:, c * JC : (c + 1) * JC],
+                    rhs=w3_w[:, b * 512 : (b + 1) * 512].bitcast(FP8X4), rhs_scale=w3_s[:, b * 512 : (b + 1) * 512],
+                    start=True, stop=True)
+                nc.scalar.copy(by_t(rain[:, c, b, :]), from_bank(acc))
+
+        soil(0, [quantize_weight("w2_%d" % i, w2_raw[i], True) for i in (0, 1)], 512)
+        v1 = [sb("v1_%d" % a, [P, S], U32) for a in range(2)]
+        for a in range(2):
+            nc.vector.tensor_copy(v1[a][:], tab_w[a][:].bitcast(U32).indirect(list1[:]))
         for b in range(2):
-            nc.vector.quantize_mx(out=wo_q[b][:].bitcast(FP8X4), scales=wo_s[b][:], in_=wo_bf[b][:])
+            accs = [bank("seed") for c in range(NC)]
+            for a in range(2):
+                col = a * H + b * 512
+                for c in range(NC):
+                    nc.tensor.matmul_mx(
+                        out=accs[c][:],
+                        lhsT=v1[a][:, c * JC : (c + 1) * JC].bitcast(FP8X4), lhsT_scale=v1_plane[:, a * S + c * JC : a * S + (c + 1) * JC],
+                        rhs=w1_w[:, 2 * col : 2 * (col + 512)].bitcast(FP4X4), rhs_scale=w1_s[:, col : col + 512],
+                        start=(a == 0), stop=(a == 1))
+            for c in range(NC):
+                nc.scalar.activation(by_t(sig_seed[:, b, c, :]), from_bank(accs[c]), ACT.Sigmoid)
+
+        soil(1, [quantize_weight("w2_%d" % i, w2_raw[i], True) for i in (2, 3)], 256)
+        both = sb("both", [P, NC, 2, 512], F32, tag="w2_raw3")
+
+        def products(b):
+            for c in range(0, NC, 2):
+                nc.vector.tensor_tensor(both[:, c : c + 2, b, :], sig_seed[:, b, c : c + 2, :], sig_soil[:, b, c : c + 2, :], ALU.mult)
+
+        products(0)
+        products(1)
+        wo_mx = [quantize_weight("wo_%d" % b, wo_raw[b], True) for b in range(2)]
+
+        logs = sb("logs", [P, NC, 2, 512], F32, tag="w2_3_q")
+        sums = {}
+        for c in range(NC):
+            for b in range(2):
+                sums[c, b] = bank("sum")
+                for t in range(4):
+                    nc.tensor.matmul(sums[c, b][:, t * JC : (t + 1) * JC], rain[:, c, b, t * P : (t + 1) * P], ident[:], start=(t == 0), stop=False, is_transpose=True)
+        for c in range(NC):
+            for b in range(2):
+                nc.scalar.activation(logs[:, c, b, :], both[:, c, b, :], ACT.Ln)
 
         out_v = out.rearrange("(m p) j -> p m j", p=P)
+        h_mx = []
+        for c in range(NC):
+            h_bf = sb("h_bf%d" % c, [P, 2, JC, 4], BF16, tag="w2_%d_bf" % c)
+            for b in range(2):
+                for t in range(4):
+                    nc.tensor.matmul(sums[c, b][:, t * JC : (t + 1) * JC], logs[:, c, b, t * P : (t + 1) * P], ident[:], start=False, stop=(t == 3), is_transpose=True)
+                nc.vector.tensor_tensor(
+                    h_bf[:, b], sums[c, b][:].rearrange("p (t j) -> p j t", t=4),
+                    gain_pt[:, b, :].unsqueeze(1).to_broadcast([P, JC, 4]), ALU.mult)
+            h_q = sb("h_q%d" % c, [P, 2 * JC], U32)
+            h_s = sb("h_s%d" % c, [P, 2 * JC], U8)
+            nc.vector.quantize_mx(out=h_q[:].bitcast(FP8X4), scales=h_s[:], in_=h_bf[:].rearrange("p b j t -> p (b j t)"))
+            h_mx.append((h_q, h_s))
+
         for c in range(NC):
             acc = bank("score")
+            h_q, h_s = h_mx[c]
             for m in range(4):
                 for b in range(2):
+                    codes, scales = wo_mx[b]
                     nc.tensor.matmul_mx(
-                        out=acc[:, m, :],
-                        lhsT=wo_q[b][:, m * P : (m + 1) * P].bitcast(FP8X4), lhsT_scale=wo_s[b][:, m * P : (m + 1) * P],
-                        rhs=h_q[c][:, b * JC : (b + 1) * JC].bitcast(FP8X4), rhs_scale=h_s[c][:, b * JC : (b + 1) * JC],
+                        out=acc[:, m * JC : (m + 1) * JC],
+                        lhsT=codes[:, m * P : (m + 1) * P].bitcast(FP8X4), lhsT_scale=scales[:, m * P : (m + 1) * P],
+                        rhs=h_q[:, b * JC : (b + 1) * JC].bitcast(FP8X4), rhs_scale=h_s[:, b * JC : (b + 1) * JC],
                         start=(b == 0), stop=(b == 1))
             res = sb("res%d" % c, [P, 4, JC], F32, tag="w2_raw%d" % c)
-            nc.scalar.copy(res[:], acc[:])
+            nc.scalar.copy(res[:].rearrange("p m j -> p (m j)"), acc[:])
             nc.sync.dma_start(out=out_v[:, :, c * JC : (c + 1) * JC], in_=res[:])

@@ -58,17 +58,13 @@ def tile_list_seed_bank_germination_kernel(
         v3_plane = sb("v3_plane", [P, S], U8)
         gain_pt = sb("gain_pt", [P, 2, 4], F32)
         ident = sb("ident", [P, P], F32)
-        warm = sb("warm", [P, 1], F32)
-        warm_out = sb("warm_out", [P, 1], F32)
 
         nc.vector.memset(tab3_s[:].bitcast(I32), 0)
         nc.vector.memset(tab_s[:].bitcast(I32), 0)
         nc.vector.memset(tab2_s[:].bitcast(I32), 0)
         nc.vector.memset(w1_s[:].bitcast(I32), 0)
-        nc.gpsimd.memset(warm[:], 0.0)
         nc.gpsimd.memset(w3_s[:].bitcast(I32), 0)
         nc.gpsimd.memset(v1_plane[:].bitcast(I32), 0)
-        nc.scalar.activation(warm_out[:], warm[:], ACT.Sigmoid)
 
         w2_raw = [sb("w2_raw%d" % i, [P, 4, 512], F32) for i in range(4)]
         wo_raw = [sb("wo_raw%d" % b, [P, 4, N], F32) for b in range(2)]
@@ -207,7 +203,7 @@ def tile_list_seed_bank_germination_kernel(
             for b in range(2):
                 sums[c, b] = bank("sum")
                 for t in range(4):
-                    nc.tensor.matmul(sums[c, b][:, t * JC : (t + 1) * JC], rain[:, c, b, t * P : (t + 1) * P], ident[:], start=(t == 0), stop=False, is_transpose=True)
+                    nc.tensor.matmul(sums[c, b][:, t : 4 * JC : 4], rain[:, c, b, t * P : (t + 1) * P], ident[:], start=(t == 0), stop=False, is_transpose=True)
         for c in range(NC):
             for b in range(2):
                 nc.scalar.activation(logs[:, c, b, :], both[:, c, b, :], ACT.Ln)
@@ -218,9 +214,9 @@ def tile_list_seed_bank_germination_kernel(
             h_bf = sb("h_bf%d" % c, [P, 2, JC, 4], BF16, tag="w2_%d_bf" % c)
             for b in range(2):
                 for t in range(4):
-                    nc.tensor.matmul(sums[c, b][:, t * JC : (t + 1) * JC], logs[:, c, b, t * P : (t + 1) * P], ident[:], start=False, stop=(t == 3), is_transpose=True)
+                    nc.tensor.matmul(sums[c, b][:, t : 4 * JC : 4], logs[:, c, b, t * P : (t + 1) * P], ident[:], start=False, stop=(t == 3), is_transpose=True)
                 nc.vector.tensor_tensor(
-                    h_bf[:, b], sums[c, b][:].rearrange("p (t j) -> p j t", t=4),
+                    h_bf[:, b], sums[c, b][:].rearrange("p (j t) -> p j t", t=4),
                     gain_pt[:, b, :].unsqueeze(1).to_broadcast([P, JC, 4]), ALU.mult)
             h_q = sb("h_q%d" % c, [P, 2 * JC], U32)
             h_s = sb("h_s%d" % c, [P, 2 * JC], U8)

@@ -66,22 +66,19 @@ def tile_list_seed_bank_germination_kernel(
         nc.gpsimd.memset(w3_s[:].bitcast(I32), 0)
         nc.gpsimd.memset(v1_plane[:].bitcast(I32), 0)
 
-        w2_raw = [sb("w2_raw%d" % i, [P, 4, 512], F32) for i in range(4)]
+        w2_pieces = [(0, 0, 512), (1, 0, 512), (0, 512, 512), (1, 512, 256), (1, 768, 256)]
+        w2_raw = [sb("w2_raw%d" % i, [P, 4, width], F32) for i, (a, c0, width) in enumerate(w2_pieces)]
         wo_raw = [sb("wo_raw%d" % b, [P, 4, N], F32) for b in range(2)]
 
         def load_w2(i):
-            b, a = divmod(i, 2)
-            nc.sync.dma_start(out=w2_raw[i][:], in_=w2[512 * a : 512 * (a + 1), 512 * b : 512 * (b + 1)].rearrange("(p j) c -> p j c", j=4))
+            a, c0, width = w2_pieces[i]
+            nc.sync.dma_start(out=w2_raw[i][:], in_=w2[512 * a : 512 * (a + 1), c0 : c0 + width].rearrange("(p j) c -> p j c", j=4))
 
         def load_tab(a):
             nc.sync.dma_start(out=tab_w[a][:], in_=tab_words[a].rearrange("p t i -> p (t i)").bitcast(I32))
 
         for q in range(4):
             nc.gpsimd.dma_start(out=w3_s[32 * q : 32 * q + 4, :].bitcast(I32), in_=w3_scales[0, 4 * q : 4 * q + 4, :].bitcast(I32))
-        for q in range(4):
-            nc.gpsimd.dma_start(
-                out=w1_s[32 * q : 32 * q + 4, :].rearrange("p (a c) -> p a c", a=2).bitcast(I32),
-                in_=w1_scales[:, 4 * q : 4 * q + 4, :].rearrange("a r c -> r a c").bitcast(I32))
         nc.sync.dma_start(out=tab3_w[:].bitcast(I32), in_=tab3_words[0].bitcast(I32))
         nc.sync.dma_start(list3[:], offs3)
         nc.sync.dma_start(out=w3_w[:], in_=w3_words[0].rearrange("p c i -> p (c i)").bitcast(I32))
@@ -91,10 +88,15 @@ def tile_list_seed_bank_germination_kernel(
         nc.sync.dma_start(list2[:], offs2)
         nc.sync.dma_start(list1[:], offs)
         nc.sync.dma_start(out=tab_s[0:P:4, :].bitcast(I32), in_=tab_scales.rearrange("a q t -> q a t").bitcast(I32))
-        load_w2(0)
+        load_tab(0)
         for q in range(4):
             nc.sync.dma_start(out=tab2_s[32 * q + TAB2_ROW : 32 * q + TAB2_ROW + 8, :].bitcast(I32), in_=tab2_scales[:, 4 * q : 4 * q + 4, :].bitcast(I32))
-        load_w2(1)
+        nc.sync.dma_start(out=w1_w[:].rearrange("p (a c) -> p a c", a=2).bitcast(I32), in_=w1_words.rearrange("a p c -> p a c").bitcast(I32))
+        for q in range(4):
+            nc.sync.dma_start(
+                out=w1_s[32 * q : 32 * q + 4, :].rearrange("p (a c) -> p a c", a=2).bitcast(I32),
+                in_=w1_scales[:, 4 * q : 4 * q + 4, :].rearrange("a r c -> r a c").bitcast(I32))
+        load_tab(1)
         v3 = sb("v3", [P, S], U16)
         nc.vector.tensor_copy(v3[:], tab3_w[:].indirect(list3[:]))
         nc.vector.tensor_copy(v3_plane[:], tab3_s[:].indirect(list3[:]))
@@ -105,31 +107,26 @@ def tile_list_seed_bank_germination_kernel(
         v1_rows = sb("v1_rows", [P, S], U8)
         nc.vector.tensor_copy(v1_rows[:], tab_s[:].indirect(list1[:]))
         nc.vector.tensor_copy(v2_plane[:], tab2_s[:].indirect(list2[:]))
-        load_tab(0)
-        nc.sync.dma_start(out=w1_w[:].rearrange("p (a c) -> p a c", a=2).bitcast(I32), in_=w1_words.rearrange("a p c -> p a c").bitcast(I32))
-        load_tab(1)
         for q in range(4):
             nc.sync.dma_start(
                 out=v1_plane[32 * q : 32 * q + 4, :].rearrange("p (a j) -> p a j", a=2).bitcast(I32),
                 in_=v1_rows[32 * q : 32 * q + 32 : 4, :].bitcast(I32))
-        load_w2(2)
+        for i in range(len(w2_pieces)):
+            load_w2(i)
         nc.sync.dma_start(out=gain_pt[:], in_=gain.rearrange("(b p t) -> p b t", b=2, t=4))
-        load_w2(3)
         for b in range(2):
             nc.sync.dma_start(out=wo_raw[b][:], in_=wo[512 * b : 512 * (b + 1), :].rearrange("(p t) n -> p t n", t=4))
 
         make_identity(nc, ident[:])
 
-        def quantize_weight(name, raw, on_vector):
-            grouped = sb(name + "_bf", [P, 4 * 512], BF16)
-            codes = sb(name + "_q", [P, 512], U32)
-            scales = sb(name + "_s", [P, 512], U8)
+        def quantize_weight(name, raw):
+            width = raw.shape[2]
+            grouped = sb(name + "_bf", [P, 4 * width], BF16)
+            codes = sb(name + "_q", [P, width], U32)
+            scales = sb(name + "_s", [P, width], U8)
             dst = grouped[:].rearrange("p (x w t) -> p x t w", w=4, t=4)
             src = raw[:].rearrange("p t (x w) -> p x t w", w=4)
-            if on_vector:
-                nc.vector.tensor_copy(dst, src)
-            else:
-                nc.scalar.copy(dst, src)
+            nc.vector.tensor_copy(dst, src)
             nc.vector.quantize_mx(out=codes[:].bitcast(FP8X4), scales=scales[:], in_=grouped[:])
             return codes, scales
 
@@ -144,16 +141,16 @@ def tile_list_seed_bank_germination_kernel(
         rain = sb("rain", [P, NC, 2, 512], F32)
 
         def soil(b, pieces, width):
-            parts = [(c, r0) for c in range(NC) for r0 in range(0, 512, width)]
+            parts = [(c, r0) for r0 in range(0, 512, width) for c in range(NC)]
             accs = [bank("soil") for part in parts]
             for a in range(2):
-                codes, scales = pieces[a]
                 row = TAB2_ROW + 4 * a
                 for acc, (c, r0) in zip(accs, parts):
+                    codes, scales = pieces[a][r0 // width]
                     nc.tensor.matmul_mx(
                         out=acc[:, 0:width],
                         lhsT=v2[a][:, c * JC : (c + 1) * JC].bitcast(FP8X4), lhsT_scale=v2_plane[row:P, c * JC : (c + 1) * JC],
-                        rhs=codes[:, r0 : r0 + width].bitcast(FP8X4), rhs_scale=scales[:, r0 : r0 + width], start=(a == 0), stop=(a == 1))
+                        rhs=codes.bitcast(FP8X4), rhs_scale=scales, start=(a == 0), stop=(a == 1))
             for acc, (c, r0) in zip(accs, parts):
                 nc.scalar.activation(
                     by_t(sig_soil[:, b, c, :])[:, :, r0 // 4 : (r0 + width) // 4],
@@ -169,7 +166,9 @@ def tile_list_seed_bank_germination_kernel(
                     start=True, stop=True)
                 nc.scalar.copy(by_t(rain[:, c, b, :]), from_bank(acc))
 
-        soil(0, [quantize_weight("w2_%d" % i, w2_raw[i], True) for i in (0, 1)], 512)
+        def columns(mx, c0, width):
+            return mx[0][:, c0 : c0 + width], mx[1][:, c0 : c0 + width]
+
         v1 = [sb("v1_%d" % a, [P, S], U32) for a in range(2)]
         for a in range(2):
             nc.vector.tensor_copy(v1[a][:], tab_w[a][:].bitcast(U32).indirect(list1[:]))
@@ -186,8 +185,10 @@ def tile_list_seed_bank_germination_kernel(
             for c in range(NC):
                 nc.scalar.activation(by_t(sig_seed[:, b, c, :]), from_bank(accs[c]), ACT.Sigmoid)
 
-        soil(1, [quantize_weight("w2_%d" % i, w2_raw[i], True) for i in (2, 3)], 256)
-        both = sb("both", [P, NC, 2, 512], F32, tag="w2_raw3")
+        soil(0, [[columns(quantize_weight("w2_%d" % i, w2_raw[i]), 0, 512)] for i in (0, 1)], 512)
+        first, low, high = [quantize_weight("w2_%d" % i, w2_raw[i]) for i in (2, 3, 4)]
+        soil(1, [[columns(first, 0, 256), columns(first, 256, 256)], [columns(low, 0, 256), columns(high, 0, 256)]], 256)
+        both = sb("both", [P, NC, 2, 512], F32, tag="w2_raw4")
 
         def products(b):
             for c in range(0, NC, 2):
@@ -195,9 +196,9 @@ def tile_list_seed_bank_germination_kernel(
 
         products(0)
         products(1)
-        wo_mx = [quantize_weight("wo_%d" % b, wo_raw[b], True) for b in range(2)]
+        wo_mx = [quantize_weight("wo_%d" % b, wo_raw[b]) for b in range(2)]
 
-        logs = sb("logs", [P, NC, 2, 512], F32, tag="w2_3_q")
+        logs = sb("logs", [P, NC, 2, 512], F32, tag="w2_4_q")
         sums = {}
         for c in range(NC):
             for b in range(2):
@@ -220,20 +221,30 @@ def tile_list_seed_bank_germination_kernel(
                     gain_pt[:, b, :].unsqueeze(1).to_broadcast([P, JC, 4]), ALU.mult)
             h_q = sb("h_q%d" % c, [P, 2 * JC], U32)
             h_s = sb("h_s%d" % c, [P, 2 * JC], U8)
-            nc.vector.quantize_mx(out=h_q[:].bitcast(FP8X4), scales=h_s[:], in_=h_bf[:].rearrange("p b j t -> p (b j t)"))
+            for b0, b1 in ([(0, 2)] if c < NC - 1 else [(0, 1), (1, 2)]):
+                nc.vector.quantize_mx(
+                    out=h_q[:, b0 * JC : b1 * JC].bitcast(FP8X4), scales=h_s[:, b0 * JC : b1 * JC],
+                    in_=h_bf[:, b0:b1].rearrange("p b j t -> p (b j t)"))
             h_mx.append((h_q, h_s))
 
         for c in range(NC):
-            acc = bank("score")
             h_q, h_s = h_mx[c]
-            for m in range(4):
-                for b in range(2):
-                    codes, scales = wo_mx[b]
-                    nc.tensor.matmul_mx(
-                        out=acc[:, m * JC : (m + 1) * JC],
-                        lhsT=codes[:, m * P : (m + 1) * P].bitcast(FP8X4), lhsT_scale=scales[:, m * P : (m + 1) * P],
-                        rhs=h_q[:, b * JC : (b + 1) * JC].bitcast(FP8X4), rhs_scale=h_s[:, b * JC : (b + 1) * JC],
-                        start=(b == 0), stop=(b == 1))
-            res = sb("res%d" % c, [P, 4, JC], F32, tag="w2_raw%d" % c)
-            nc.scalar.copy(res[:].rearrange("p m j -> p (m j)"), acc[:])
-            nc.sync.dma_start(out=out_v[:, :, c * JC : (c + 1) * JC], in_=res[:])
+            groups = [range(4)] if c < NC - 1 else [range(0, 2), range(2, 4)]
+            accs = [bank("score") for ms in groups]
+            for b in range(2):
+                codes, scales = wo_mx[b]
+                for acc, ms in zip(accs, groups):
+                    for i, m in enumerate(ms):
+                        nc.tensor.matmul_mx(
+                            out=acc[:, i * JC : (i + 1) * JC],
+                            lhsT=codes[:, m * P : (m + 1) * P].bitcast(FP8X4), lhsT_scale=scales[:, m * P : (m + 1) * P],
+                            rhs=h_q[:, b * JC : (b + 1) * JC].bitcast(FP8X4), rhs_scale=h_s[:, b * JC : (b + 1) * JC],
+                            start=(b == 0 and i == 0), stop=(b == 1 and i == len(ms) - 1))
+            for g, (acc, ms) in enumerate(zip(accs, groups)):
+                res = sb("res%d%d" % (c, g), [P, len(ms), JC], F32)
+                flat = res[:].rearrange("p m j -> p (m j)")
+                if g == 0:
+                    nc.scalar.copy(flat, acc[:, 0 : len(ms) * JC])
+                else:
+                    nc.vector.tensor_copy(flat, acc[:, 0 : len(ms) * JC])
+                nc.sync.dma_start(out=out_v[:, ms.start : ms.stop, c * JC : (c + 1) * JC], in_=res[:])

@@ -188,17 +188,17 @@ def tile_list_seed_bank_germination_kernel(
         soil(0, [[columns(quantize_weight("w2_%d" % i, w2_raw[i]), 0, 512)] for i in (0, 1)], 512)
         first, low, high = [quantize_weight("w2_%d" % i, w2_raw[i]) for i in (2, 3, 4)]
         soil(1, [[columns(first, 0, 256), columns(first, 256, 256)], [columns(low, 0, 256), columns(high, 0, 256)]], 256)
-        both = sb("both", [P, NC, 2, 512], F32, tag="w2_raw4")
+        both = sb("both", [P, NC + 2, 512], F32, tag="w2_raw4")
 
         def products(b):
             for c in range(0, NC, 2):
-                nc.vector.tensor_tensor(both[:, c : c + 2, b, :], sig_seed[:, b, c : c + 2, :], sig_soil[:, b, c : c + 2, :], ALU.mult)
+                nc.vector.tensor_tensor(both[:, c : c + 2, :], sig_seed[:, b, c : c + 2, :], sig_soil[:, b, c : c + 2, :], ALU.mult)
 
         products(0)
-        products(1)
+        nc.vector.tensor_tensor(both[:, NC : NC + 2, :], sig_seed[:, 1, 2:4, :], sig_soil[:, 1, 2:4, :], ALU.mult)
         wo_mx = [quantize_weight("wo_%d" % b, wo_raw[b]) for b in range(2)]
 
-        logs = sb("logs", [P, NC, 2, 512], F32, tag="w2_4_q")
+        logs = sb("logs", [P, NC, 3, 512], F32, tag="w2_4_q")
         sums = {}
         for c in range(NC):
             for b in range(2):
@@ -206,16 +206,24 @@ def tile_list_seed_bank_germination_kernel(
                 for t in range(4):
                     nc.tensor.matmul(sums[c, b][:, t : 4 * JC : 4], rain[:, c, b, t * P : (t + 1) * P], ident[:], start=(t == 0), stop=False, is_transpose=True)
         for c in range(NC):
-            for b in range(2):
-                nc.scalar.activation(logs[:, c, b, :], both[:, c, b, :], ACT.Ln)
+            nc.scalar.activation(logs[:, c, 0, :], both[:, c, :], ACT.Ln)
+            if c < 2:
+                nc.scalar.activation(logs[:, c, 1, :], sig_seed[:, 1, c, :], ACT.Ln)
+                nc.scalar.activation(logs[:, c, 2, :], sig_soil[:, 1, c, :], ACT.Ln)
+            else:
+                nc.scalar.activation(logs[:, c, 1, :], both[:, NC + c - 2, :], ACT.Ln)
 
         out_v = out.rearrange("(m p) j -> p m j", p=P)
         h_mx = []
         for c in range(NC):
             h_bf = sb("h_bf%d" % c, [P, 2, JC, 4], BF16, tag="w2_%d_bf" % c)
             for b in range(2):
-                for t in range(4):
-                    nc.tensor.matmul(sums[c, b][:, t : 4 * JC : 4], logs[:, c, b, t * P : (t + 1) * P], ident[:], start=False, stop=(t == 3), is_transpose=True)
+                terms = [(0,), (1, 2) if c < 2 else (1,)][b]
+                for term in terms:
+                    for t in range(4):
+                        nc.tensor.matmul(
+                            sums[c, b][:, t : 4 * JC : 4], logs[:, c, term, t * P : (t + 1) * P], ident[:],
+                            start=False, stop=(t == 3 and term == terms[-1]), is_transpose=True)
                 nc.vector.tensor_tensor(
                     h_bf[:, b], sums[c, b][:].rearrange("p (j t) -> p j t", t=4),
                     gain_pt[:, b, :].unsqueeze(1).to_broadcast([P, JC, 4]), ALU.mult)

@@ -20,7 +20,6 @@ ALU = mybir.AluOpType
 P = 128
 JC = 128
 NC = S // JC
-TAB2_ROW = 8
 
 
 def tile_list_seed_bank_germination_kernel(
@@ -31,14 +30,12 @@ def tile_list_seed_bank_germination_kernel(
     with ExitStack() as ctx:
         keep = ctx.enter_context(tc.tile_pool(name="keep", bufs=1))
         psum = ctx.enter_context(tc.psum_pool(name="psum", bufs=1))
-        taken = []
 
         def sb(name, shape, dtype, tag=None):
             return keep.tile(shape, dtype, name=name, tag=tag or name, align_bytes=64)
 
-        def bank(name):
-            taken.append(name)
-            return psum.tile([P, 512], F32, name=name, tag="bank%d" % ((len(taken) - 1) % 8))
+        def bank(name, number):
+            return psum.tile([P, 512], F32, name=name, tag="bank%d" % number)
 
         list1 = keep.tile([P, S // 16], U16, name="list1")
         list2 = keep.tile([P, S // 16], U16, name="list2")
@@ -46,7 +43,7 @@ def tile_list_seed_bank_germination_kernel(
 
         tab_w = [sb("tab_w%d" % a, [P, T1], I32) for a in range(2)]
         tab_s = sb("tab_s", [P, T1], U8)
-        tab2_w = sb("tab2_w", [P, 2 * T2], I32)
+        tab2_w = [sb("tab2_w%d" % a, [P, T2], I32) for a in range(2)]
         tab2_s = sb("tab2_s", [P, T2], U8)
         tab3_w = sb("tab3_w", [P, T3], U16)
         tab3_s = sb("tab3_s", [P, T3], U8)
@@ -54,7 +51,7 @@ def tile_list_seed_bank_germination_kernel(
         w1_s = sb("w1_s", [P, 2 * H], U8)
         w3_w = sb("w3_w", [P, H], I32)
         w3_s = sb("w3_s", [P, H], U8)
-        v1_plane = sb("v1_plane", [P, 2 * S], U8)
+        planes = sb("planes", [P, 4 * S], U8)
         v3_plane = sb("v3_plane", [P, S], U8)
         gain_pt = sb("gain_pt", [P, 2, 4], F32)
         ident = sb("ident", [P, P], F32)
@@ -63,8 +60,8 @@ def tile_list_seed_bank_germination_kernel(
         nc.vector.memset(tab_s[:].bitcast(I32), 0)
         nc.vector.memset(tab2_s[:].bitcast(I32), 0)
         nc.vector.memset(w1_s[:].bitcast(I32), 0)
+        nc.vector.memset(planes[:].bitcast(I32), 0)
         nc.gpsimd.memset(w3_s[:].bitcast(I32), 0)
-        nc.gpsimd.memset(v1_plane[:].bitcast(I32), 0)
 
         w2_pieces = [(0, 0, 512), (1, 0, 512), (0, 512, 512), (1, 512, 256), (1, 768, 256)]
         w2_raw = [sb("w2_raw%d" % i, [P, 4, width], F32) for i, (a, c0, width) in enumerate(w2_pieces)]
@@ -77,40 +74,39 @@ def tile_list_seed_bank_germination_kernel(
         def load_tab(a):
             nc.sync.dma_start(out=tab_w[a][:], in_=tab_words[a].rearrange("p t i -> p (t i)").bitcast(I32))
 
+        def load_tab2(a):
+            nc.sync.dma_start(out=tab2_w[a][:], in_=tab2_words[a].rearrange("p t i -> p (t i)").bitcast(I32))
+
         for q in range(4):
             nc.gpsimd.dma_start(out=w3_s[32 * q : 32 * q + 4, :].bitcast(I32), in_=w3_scales[0, 4 * q : 4 * q + 4, :].bitcast(I32))
-        nc.sync.dma_start(out=tab3_w[:].bitcast(I32), in_=tab3_words[0].bitcast(I32))
         nc.sync.dma_start(list3[:], offs3)
-        nc.sync.dma_start(out=w3_w[:], in_=w3_words[0].rearrange("p c i -> p (c i)").bitcast(I32))
+        nc.sync.dma_start(out=tab3_w[:].bitcast(I32), in_=tab3_words[0].bitcast(I32))
         for q in range(4):
             nc.sync.dma_start(out=tab3_s[32 * q : 32 * q + 4, :].bitcast(I32), in_=tab3_scales[0, 4 * q : 4 * q + 4, :].bitcast(I32))
-        nc.sync.dma_start(out=tab2_w[:].rearrange("p (a t) -> p a t", a=2), in_=tab2_words.rearrange("a p t i -> p a (t i)").bitcast(I32))
-        nc.sync.dma_start(list2[:], offs2)
+        nc.sync.dma_start(out=w3_w[:], in_=w3_words[0].rearrange("p c i -> p (c i)").bitcast(I32))
+        load_tab(0)
         nc.sync.dma_start(list1[:], offs)
         nc.sync.dma_start(out=tab_s[0:P:4, :].bitcast(I32), in_=tab_scales.rearrange("a q t -> q a t").bitcast(I32))
-        load_tab(0)
-        for q in range(4):
-            nc.sync.dma_start(out=tab2_s[32 * q + TAB2_ROW : 32 * q + TAB2_ROW + 8, :].bitcast(I32), in_=tab2_scales[:, 4 * q : 4 * q + 4, :].bitcast(I32))
-        nc.sync.dma_start(out=w1_w[:].rearrange("p (a c) -> p a c", a=2).bitcast(I32), in_=w1_words.rearrange("a p c -> p a c").bitcast(I32))
+        nc.sync.dma_start(list2[:], offs2)
+        nc.sync.dma_start(out=tab2_s[0:P:4, :].bitcast(I32), in_=tab2_scales.rearrange("a q t -> q a t").bitcast(I32))
+        load_tab(1)
         for q in range(4):
             nc.sync.dma_start(
                 out=w1_s[32 * q : 32 * q + 4, :].rearrange("p (a c) -> p a c", a=2).bitcast(I32),
                 in_=w1_scales[:, 4 * q : 4 * q + 4, :].rearrange("a r c -> r a c").bitcast(I32))
-        load_tab(1)
+        nc.sync.dma_start(out=w1_w[:].rearrange("p (a c) -> p a c", a=2).bitcast(I32), in_=w1_words.rearrange("a p c -> p a c").bitcast(I32))
+        load_tab2(0)
         v3 = sb("v3", [P, S], U16)
+        rows = sb("rows", [P, 2 * S], U8)
         nc.vector.tensor_copy(v3[:], tab3_w[:].indirect(list3[:]))
         nc.vector.tensor_copy(v3_plane[:], tab3_s[:].indirect(list3[:]))
-        v2 = [sb("v2_%d" % a, [P, S], U32) for a in range(2)]
-        v2_plane = sb("v2_plane", [P, S], U8)
-        nc.vector.tensor_copy(v2[0][:], tab2_w[:, 0:T2].bitcast(U32).indirect(list2[:]))
-        nc.vector.tensor_copy(v2[1][:], tab2_w[:, T2 : 2 * T2].bitcast(U32).indirect(list2[:]))
-        v1_rows = sb("v1_rows", [P, S], U8)
-        nc.vector.tensor_copy(v1_rows[:], tab_s[:].indirect(list1[:]))
-        nc.vector.tensor_copy(v2_plane[:], tab2_s[:].indirect(list2[:]))
+        nc.vector.tensor_copy(rows[:, 0:S], tab_s[:].indirect(list1[:]))
+        nc.vector.tensor_copy(rows[:, S : 2 * S], tab2_s[:].indirect(list2[:]))
         for q in range(4):
             nc.sync.dma_start(
-                out=v1_plane[32 * q : 32 * q + 4, :].rearrange("p (a j) -> p a j", a=2).bitcast(I32),
-                in_=v1_rows[32 * q : 32 * q + 32 : 4, :].bitcast(I32))
+                out=planes[32 * q : 32 * q + 4, :].rearrange("p (a j) -> p a j", a=2).bitcast(I32),
+                in_=rows[32 * q : 32 * q + 32 : 4, :].bitcast(I32))
+        load_tab2(1)
         for i in range(len(w2_pieces)):
             load_w2(i)
         nc.sync.dma_start(out=gain_pt[:], in_=gain.rearrange("(b p t) -> p b t", b=2, t=4))
@@ -140,25 +136,31 @@ def tile_list_seed_bank_germination_kernel(
         sig_seed = sb("sig_seed", [P, 2, NC, 512], F32)
         rain = sb("rain", [P, NC, 2, 512], F32)
 
-        def soil(b, pieces, width):
-            parts = [(c, r0) for r0 in range(0, 512, width) for c in range(NC)]
-            accs = [bank("soil") for part in parts]
-            for a in range(2):
-                row = TAB2_ROW + 4 * a
-                for acc, (c, r0) in zip(accs, parts):
-                    codes, scales = pieces[a][r0 // width]
+        def soil(b, r0, width, pieces, first_bank):
+            share = 512 // width
+            accs = [bank("soil", first_bank + i) for i in range(NC // share)]
+
+            def passes(order):
+                for a, c in order:
+                    col = (2 * a + 1) * S
+                    codes, scales = pieces[a]
+                    i = c % share
                     nc.tensor.matmul_mx(
-                        out=acc[:, 0:width],
-                        lhsT=v2[a][:, c * JC : (c + 1) * JC].bitcast(FP8X4), lhsT_scale=v2_plane[row:P, c * JC : (c + 1) * JC],
-                        rhs=codes.bitcast(FP8X4), rhs_scale=scales, start=(a == 0), stop=(a == 1))
-            for acc, (c, r0) in zip(accs, parts):
-                nc.scalar.activation(
-                    by_t(sig_soil[:, b, c, :])[:, :, r0 // 4 : (r0 + width) // 4],
-                    acc[:, 0:width].rearrange("j (p t) -> j t p", t=4), ACT.Sigmoid)
+                        out=accs[c // share][:, i * width : (i + 1) * width],
+                        lhsT=v2[a][:, c * JC : (c + 1) * JC].bitcast(FP8X4), lhsT_scale=planes[:, col + c * JC : col + (c + 1) * JC],
+                        rhs=codes.bitcast(FP8X4), rhs_scale=scales, start=(a == 0 and i == 0), stop=(a == 1 and i == share - 1))
+
+            def sigmoids():
+                for i, acc in enumerate(accs):
+                    nc.scalar.activation(
+                        sig_soil[:, b, i * share : (i + 1) * share, :].rearrange("j c (t p) -> j c t p", t=4)[:, :, :, r0 // 4 : (r0 + width) // 4],
+                        acc[:].rearrange("j (c p t) -> j c t p", c=share, t=4), ACT.Sigmoid)
+
+            return passes, sigmoids
 
         for c in range(NC):
             for b in range(2):
-                acc = bank("rain")
+                acc = bank("rain", 2 * c + b)
                 nc.tensor.matmul_mx(
                     out=acc[:],
                     lhsT=v3[:, c * JC : (c + 1) * JC].bitcast(FP4X4), lhsT_scale=v3_plane[:, c * JC : (c + 1) * JC],
@@ -170,25 +172,36 @@ def tile_list_seed_bank_germination_kernel(
             return mx[0][:, c0 : c0 + width], mx[1][:, c0 : c0 + width]
 
         v1 = [sb("v1_%d" % a, [P, S], U32) for a in range(2)]
+        v2 = [sb("v2_%d" % a, [P, S], U32) for a in range(2)]
         for a in range(2):
             nc.vector.tensor_copy(v1[a][:], tab_w[a][:].bitcast(U32).indirect(list1[:]))
+        for a in range(2):
+            nc.vector.tensor_copy(v2[a][:], tab2_w[a][:].bitcast(U32).indirect(list2[:]))
         for b in range(2):
-            accs = [bank("seed") for c in range(NC)]
-            for a in range(2):
-                col = a * H + b * 512
-                for c in range(NC):
+            accs = [bank("seed", 4 * b + c) for c in range(NC)]
+            for c in range(NC):
+                for a in range(2):
+                    col = a * H + b * 512
                     nc.tensor.matmul_mx(
                         out=accs[c][:],
-                        lhsT=v1[a][:, c * JC : (c + 1) * JC].bitcast(FP8X4), lhsT_scale=v1_plane[:, a * S + c * JC : a * S + (c + 1) * JC],
+                        lhsT=v1[a][:, c * JC : (c + 1) * JC].bitcast(FP8X4), lhsT_scale=planes[:, 2 * a * S + c * JC : 2 * a * S + (c + 1) * JC],
                         rhs=w1_w[:, 2 * col : 2 * (col + 512)].bitcast(FP4X4), rhs_scale=w1_s[:, col : col + 512],
                         start=(a == 0), stop=(a == 1))
             for c in range(NC):
                 nc.scalar.activation(by_t(sig_seed[:, b, c, :]), from_bank(accs[c]), ACT.Sigmoid)
 
-        soil(0, [[columns(quantize_weight("w2_%d" % i, w2_raw[i]), 0, 512)] for i in (0, 1)], 512)
+        passes, sigmoids = soil(0, 0, 512, [columns(quantize_weight("w2_%d" % i, w2_raw[i]), 0, 512) for i in (0, 1)], 4)
+        passes([(a, c) for c in range(NC) for a in range(2)])
+        sigmoids()
         first, low, high = [quantize_weight("w2_%d" % i, w2_raw[i]) for i in (2, 3, 4)]
-        soil(1, [[columns(first, 0, 256), columns(first, 256, 256)], [columns(low, 0, 256), columns(high, 0, 256)]], 256)
-        both = sb("both", [P, NC + 2, 512], F32, tag="w2_raw4")
+        parts = [
+            soil(1, 0, 256, [columns(first, 0, 256), columns(low, 0, 256)], 4),
+            soil(1, 256, 256, [columns(first, 256, 256), columns(high, 0, 256)], 6)]
+        for passes, sigmoids in parts:
+            passes([(a, c) for a in range(2) for c in range(NC)])
+        for passes, sigmoids in parts:
+            sigmoids()
+        both = sb("both", [P, NC + 2, 512], F32, tag="w2_4_bf")
 
         def products(b):
             for c in range(0, NC, 2):
@@ -198,20 +211,21 @@ def tile_list_seed_bank_germination_kernel(
         nc.vector.tensor_tensor(both[:, NC : NC + 2, :], sig_seed[:, 1, 2:4, :], sig_soil[:, 1, 2:4, :], ALU.mult)
         wo_mx = [quantize_weight("wo_%d" % b, wo_raw[b]) for b in range(2)]
 
-        logs = sb("logs", [P, NC, 3, 512], F32, tag="w2_4_q")
+        logs = sb("logs", [P, 2 * NC + 2, 512], F32, tag="w2_4_q")
+        first_log = [0, 3, 6, 8]
         sums = {}
-        for c in range(NC):
-            for b in range(2):
-                sums[c, b] = bank("sum")
+        for b in range(2):
+            for c in range(NC):
+                sums[c, b] = bank("sum", 4 * b + c)
                 for t in range(4):
                     nc.tensor.matmul(sums[c, b][:, t : 4 * JC : 4], rain[:, c, b, t * P : (t + 1) * P], ident[:], start=(t == 0), stop=False, is_transpose=True)
         for c in range(NC):
-            nc.scalar.activation(logs[:, c, 0, :], both[:, c, :], ACT.Ln)
+            nc.scalar.activation(logs[:, first_log[c] + 0, :], both[:, c, :], ACT.Ln)
             if c < 2:
-                nc.scalar.activation(logs[:, c, 1, :], sig_seed[:, 1, c, :], ACT.Ln)
-                nc.scalar.activation(logs[:, c, 2, :], sig_soil[:, 1, c, :], ACT.Ln)
+                nc.scalar.activation(logs[:, first_log[c] + 1, :], sig_seed[:, 1, c, :], ACT.Ln)
+                nc.scalar.activation(logs[:, first_log[c] + 2, :], sig_soil[:, 1, c, :], ACT.Ln)
             else:
-                nc.scalar.activation(logs[:, c, 1, :], both[:, NC + c - 2, :], ACT.Ln)
+                nc.scalar.activation(logs[:, first_log[c] + 1, :], both[:, NC + c - 2, :], ACT.Ln)
 
         out_v = out.rearrange("(m p) j -> p m j", p=P)
         h_mx = []
@@ -222,7 +236,7 @@ def tile_list_seed_bank_germination_kernel(
                 for term in terms:
                     for t in range(4):
                         nc.tensor.matmul(
-                            sums[c, b][:, t : 4 * JC : 4], logs[:, c, term, t * P : (t + 1) * P], ident[:],
+                            sums[c, b][:, t : 4 * JC : 4], logs[:, first_log[c] + term, t * P : (t + 1) * P], ident[:],
                             start=False, stop=(t == 3 and term == terms[-1]), is_transpose=True)
                 nc.vector.tensor_tensor(
                     h_bf[:, b], sums[c, b][:].rearrange("p (j t) -> p j t", t=4),
@@ -238,7 +252,7 @@ def tile_list_seed_bank_germination_kernel(
         for c in range(NC):
             h_q, h_s = h_mx[c]
             groups = [range(4)] if c < NC - 1 else [range(0, 2), range(2, 4)]
-            accs = [bank("score") for ms in groups]
+            accs = [bank("score", c + g) for g in range(len(groups))]
             for b in range(2):
                 codes, scales = wo_mx[b]
                 for acc, ms in zip(accs, groups):

@@ -78,11 +78,11 @@ def tile_list_seed_bank_germination_kernel(
             nc.sync.dma_start(out=tab2_w[a][:], in_=tab2_words[a].rearrange("p t i -> p (t i)").bitcast(I32))
 
         for q in range(4):
-            nc.gpsimd.dma_start(out=w3_s[32 * q : 32 * q + 4, :].bitcast(I32), in_=w3_scales[0, 4 * q : 4 * q + 4, :].bitcast(I32))
+            nc.gpsimd.dma_start(out=w3_s[q:P:32, :].bitcast(I32), in_=w3_scales[0, q:16:4, :].bitcast(I32))
         nc.sync.dma_start(list3[:], offs3)
         nc.sync.dma_start(out=tab3_w[:].bitcast(I32), in_=tab3_words[0].bitcast(I32))
         for q in range(4):
-            nc.sync.dma_start(out=tab3_s[32 * q : 32 * q + 4, :].bitcast(I32), in_=tab3_scales[0, 4 * q : 4 * q + 4, :].bitcast(I32))
+            nc.sync.dma_start(out=tab3_s[q:P:32, :].bitcast(I32), in_=tab3_scales[0, q:16:4, :].bitcast(I32))
         nc.sync.dma_start(out=w3_w[:], in_=w3_words[0].rearrange("p c i -> p (c i)").bitcast(I32))
         load_tab(0)
         nc.sync.dma_start(list1[:], offs)
@@ -92,8 +92,8 @@ def tile_list_seed_bank_germination_kernel(
         load_tab(1)
         for q in range(4):
             nc.sync.dma_start(
-                out=w1_s[32 * q : 32 * q + 4, :].rearrange("p (a c) -> p a c", a=2).bitcast(I32),
-                in_=w1_scales[:, 4 * q : 4 * q + 4, :].rearrange("a r c -> r a c").bitcast(I32))
+                out=w1_s[q:P:32, :].rearrange("p (a c) -> p a c", a=2).bitcast(I32),
+                in_=w1_scales[:, q:16:4, :].rearrange("a r c -> r a c").bitcast(I32))
         nc.sync.dma_start(out=w1_w[:].rearrange("p (a c) -> p a c", a=2).bitcast(I32), in_=w1_words.rearrange("a p c -> p a c").bitcast(I32))
         load_tab2(0)
         v3 = sb("v3", [P, S], U16)
@@ -102,7 +102,7 @@ def tile_list_seed_bank_germination_kernel(
         nc.vector.tensor_copy(v3_plane[:], tab3_s[:].indirect(list3[:]))
         nc.vector.tensor_copy(rows[:, 0:S], tab_s[:].indirect(list1[:]))
         nc.vector.tensor_copy(rows[:, S : 2 * S], tab2_s[:].indirect(list2[:]))
-        for q in range(4):
+        for q in (0, 2, 1, 3):
             nc.sync.dma_start(
                 out=planes[32 * q : 32 * q + 4, :].rearrange("p (a j) -> p a j", a=2).bitcast(I32),
                 in_=rows[32 * q : 32 * q + 32 : 4, :].bitcast(I32))

@@ -20,6 +20,7 @@ ALU = mybir.AluOpType
 P = 128
 JC = 128
 NC = S // JC
+APART = 1
 
 
 def tile_list_seed_bank_germination_kernel(
@@ -47,35 +48,40 @@ def tile_list_seed_bank_germination_kernel(
         tab2_s = sb("tab2_s", [P, T2], U8)
         tab3_w = sb("tab3_w", [P, T3], U16)
         tab3_s = sb("tab3_s", [P, T3], U8)
-        w1_w = sb("w1_w", [P, 4 * H], U8)
+        w1_w = [sb("w1_w%d" % b, [P, 2, H], U8) for b in range(2)]
         w1_s = sb("w1_s", [P, 2 * H], U8)
         w3_w = sb("w3_w", [P, H], I32)
         w3_s = sb("w3_s", [P, H], U8)
-        planes = sb("planes", [P, 4 * S], U8)
+        planes = sb("planes", [P, 2 * S], U8)
+        v2_planes = sb("v2_planes", [P, S], U8)
         v3_plane = sb("v3_plane", [P, S], U8)
         gain_pt = sb("gain_pt", [P, 2, 4], F32)
         ident = sb("ident", [P, P], F32)
 
         nc.vector.memset(tab3_s[:].bitcast(I32), 0)
         nc.vector.memset(tab_s[:].bitcast(I32), 0)
-        nc.vector.memset(tab2_s[:].bitcast(I32), 0)
         nc.vector.memset(w1_s[:].bitcast(I32), 0)
         nc.vector.memset(planes[:].bitcast(I32), 0)
+        nc.vector.memset(tab2_s[:].bitcast(I32), 0)
+        warm = sb("warm", [P, 2], F32)
+        nc.gpsimd.memset(warm[:, 0:1], 0.0)
+        nc.scalar.activation(warm[:, 1:2], warm[:, 0:1], ACT.Sigmoid)
         nc.gpsimd.memset(w3_s[:].bitcast(I32), 0)
 
         w2_pieces = [(0, 0, 512), (1, 0, 512), (0, 512, 512), (1, 512, 256), (1, 768, 256)]
         w2_raw = [sb("w2_raw%d" % i, [P, 4, width], F32) for i, (a, c0, width) in enumerate(w2_pieces)]
-        wo_raw = [sb("wo_raw%d" % b, [P, 4, N], F32) for b in range(2)]
+        wo_pieces = [(0, 0, 256), (0, 256, 256), (1, 0, 512)]
+        wo_raw = [sb("wo_raw%d" % i, [P, 4, width], F32) for i, (b, n0, width) in enumerate(wo_pieces)]
 
         def load_w2(i):
             a, c0, width = w2_pieces[i]
             nc.sync.dma_start(out=w2_raw[i][:], in_=w2[512 * a : 512 * (a + 1), c0 : c0 + width].rearrange("(p j) c -> p j c", j=4))
 
-        def load_tab(a):
-            nc.sync.dma_start(out=tab_w[a][:], in_=tab_words[a].rearrange("p t i -> p (t i)").bitcast(I32))
+        def load_words(tile, words):
+            nc.sync.dma_start(out=tile[:], in_=words.rearrange("p t i -> p (t i)").bitcast(I32))
 
-        def load_tab2(a):
-            nc.sync.dma_start(out=tab2_w[a][:], in_=tab2_words[a].rearrange("p t i -> p (t i)").bitcast(I32))
+        def load_w1(b):
+            nc.sync.dma_start(out=w1_w[b][:].bitcast(I32), in_=w1_words[:, :, b * H : (b + 1) * H].rearrange("a p c -> p a c").bitcast(I32))
 
         for q in range(4):
             nc.gpsimd.dma_start(out=w3_s[q:P:32, :].bitcast(I32), in_=w3_scales[0, q:16:4, :].bitcast(I32))
@@ -83,48 +89,58 @@ def tile_list_seed_bank_germination_kernel(
         nc.sync.dma_start(out=tab3_w[:].bitcast(I32), in_=tab3_words[0].bitcast(I32))
         for q in range(4):
             nc.sync.dma_start(out=tab3_s[q:P:32, :].bitcast(I32), in_=tab3_scales[0, q:16:4, :].bitcast(I32))
-        nc.sync.dma_start(out=w3_w[:], in_=w3_words[0].rearrange("p c i -> p (c i)").bitcast(I32))
-        load_tab(0)
+        load_words(w3_w, w3_words[0])
         nc.sync.dma_start(list1[:], offs)
         nc.sync.dma_start(out=tab_s[0:P:4, :].bitcast(I32), in_=tab_scales.rearrange("a q t -> q a t").bitcast(I32))
-        nc.sync.dma_start(list2[:], offs2)
-        nc.sync.dma_start(out=tab2_s[0:P:4, :].bitcast(I32), in_=tab2_scales.rearrange("a q t -> q a t").bitcast(I32))
-        load_tab(1)
+        load_words(tab_w[0], tab_words[0])
         for q in range(4):
             nc.sync.dma_start(
                 out=w1_s[q:P:32, :].rearrange("p (a c) -> p a c", a=2).bitcast(I32),
                 in_=w1_scales[:, q:16:4, :].rearrange("a r c -> r a c").bitcast(I32))
-        nc.sync.dma_start(out=w1_w[:].rearrange("p (a c) -> p a c", a=2).bitcast(I32), in_=w1_words.rearrange("a p c -> p a c").bitcast(I32))
-        load_tab2(0)
+        load_w1(0)
+        load_words(tab_w[1], tab_words[1])
         v3 = sb("v3", [P, S], U16)
-        rows = sb("rows", [P, 2 * S], U8)
+        rows = sb("rows", [P, S], U8)
         nc.vector.tensor_copy(v3[:], tab3_w[:].indirect(list3[:]))
         nc.vector.tensor_copy(v3_plane[:], tab3_s[:].indirect(list3[:]))
-        nc.vector.tensor_copy(rows[:, 0:S], tab_s[:].indirect(list1[:]))
-        nc.vector.tensor_copy(rows[:, S : 2 * S], tab2_s[:].indirect(list2[:]))
+        nc.vector.tensor_copy(rows[:], tab_s[:].indirect(list1[:]))
         for q in (0, 2, 1, 3):
             nc.sync.dma_start(
                 out=planes[32 * q : 32 * q + 4, :].rearrange("p (a j) -> p a j", a=2).bitcast(I32),
                 in_=rows[32 * q : 32 * q + 32 : 4, :].bitcast(I32))
-        load_tab2(1)
+        nc.sync.dma_start(list2[:], offs2)
+        load_w1(1)
+        for a in range(2):
+            load_words(tab2_w[a], tab2_words[a])
+        for q in range(4):
+            nc.sync.dma_start(out=tab2_s[32 * q + 4 : 32 * q + 12, :].bitcast(I32), in_=tab2_scales[:, 4 * q : 4 * q + 4, :].bitcast(I32))
         for i in range(len(w2_pieces)):
             load_w2(i)
         nc.sync.dma_start(out=gain_pt[:], in_=gain.rearrange("(b p t) -> p b t", b=2, t=4))
-        for b in range(2):
-            nc.sync.dma_start(out=wo_raw[b][:], in_=wo[512 * b : 512 * (b + 1), :].rearrange("(p t) n -> p t n", t=4))
+        for i, (b, n0, width) in enumerate(wo_pieces):
+            nc.sync.dma_start(out=wo_raw[i][:], in_=wo[512 * b : 512 * (b + 1), n0 : n0 + width].rearrange("(p t) n -> p t n", t=4))
 
         make_identity(nc, ident[:])
 
-        def quantize_weight(name, raw):
-            width = raw.shape[2]
-            grouped = sb(name + "_bf", [P, 4 * width], BF16)
-            codes = sb(name + "_q", [P, width], U32)
-            scales = sb(name + "_s", [P, width], U8)
+        def round_weight(name, raw):
+            grouped = sb(name + "_bf", [P, 4 * raw.shape[2]], BF16)
             dst = grouped[:].rearrange("p (x w t) -> p x t w", w=4, t=4)
             src = raw[:].rearrange("p t (x w) -> p x t w", w=4)
             nc.vector.tensor_copy(dst, src)
+            return grouped
+
+        def quantize(name, grouped):
+            width = grouped.shape[1] // 4
+            codes = sb(name + "_q", [P, width], U32)
+            scales = sb(name + "_s", [P, width], U8)
             nc.vector.quantize_mx(out=codes[:].bitcast(FP8X4), scales=scales[:], in_=grouped[:])
             return codes, scales
+
+        def quantize_weight(name, raw):
+            return quantize(name, round_weight(name, raw))
+
+        def columns(mx, c0, width):
+            return mx[0][:, c0 : c0 + width], mx[1][:, c0 : c0 + width]
 
         def by_t(ap):
             return ap.rearrange("j (t p) -> j t p", t=4)
@@ -132,31 +148,9 @@ def tile_list_seed_bank_germination_kernel(
         def from_bank(acc):
             return acc[:].rearrange("j (p t) -> j t p", t=4)
 
-        sig_soil = sb("sig_soil", [P, 2, NC, 512], F32)
-        sig_seed = sb("sig_seed", [P, 2, NC, 512], F32)
-        rain = sb("rain", [P, NC, 2, 512], F32)
-
-        def soil(b, r0, width, pieces, first_bank):
-            share = 512 // width
-            accs = [bank("soil", first_bank + i) for i in range(NC // share)]
-
-            def passes(order):
-                for a, c in order:
-                    col = (2 * a + 1) * S
-                    codes, scales = pieces[a]
-                    i = c % share
-                    nc.tensor.matmul_mx(
-                        out=accs[c // share][:, i * width : (i + 1) * width],
-                        lhsT=v2[a][:, c * JC : (c + 1) * JC].bitcast(FP8X4), lhsT_scale=planes[:, col + c * JC : col + (c + 1) * JC],
-                        rhs=codes.bitcast(FP8X4), rhs_scale=scales, start=(a == 0 and i == 0), stop=(a == 1 and i == share - 1))
-
-            def sigmoids():
-                for i, acc in enumerate(accs):
-                    nc.scalar.activation(
-                        sig_soil[:, b, i * share : (i + 1) * share, :].rearrange("j c (t p) -> j c t p", t=4)[:, :, :, r0 // 4 : (r0 + width) // 4],
-                        acc[:].rearrange("j (c p t) -> j c t p", c=share, t=4), ACT.Sigmoid)
-
-            return passes, sigmoids
+        sig_seed = [sb("sig_seed%d" % b, [P, NC, 512], F32) for b in range(2)]
+        sig_soil = [sb("sig_soil%d" % b, [P, NC, 512], F32) for b in range(2)]
+        rain = [sb("rain%d" % b, [P, NC, 512], F32) for b in range(2)]
 
         for c in range(NC):
             for b in range(2):
@@ -166,32 +160,74 @@ def tile_list_seed_bank_germination_kernel(
                     lhsT=v3[:, c * JC : (c + 1) * JC].bitcast(FP4X4), lhsT_scale=v3_plane[:, c * JC : (c + 1) * JC],
                     rhs=w3_w[:, b * 512 : (b + 1) * 512].bitcast(FP8X4), rhs_scale=w3_s[:, b * 512 : (b + 1) * 512],
                     start=True, stop=True)
-                nc.scalar.copy(by_t(rain[:, c, b, :]), from_bank(acc))
-
-        def columns(mx, c0, width):
-            return mx[0][:, c0 : c0 + width], mx[1][:, c0 : c0 + width]
+                nc.scalar.copy(by_t(rain[b][:, c, :]), from_bank(acc))
 
         v1 = [sb("v1_%d" % a, [P, S], U32) for a in range(2)]
         v2 = [sb("v2_%d" % a, [P, S], U32) for a in range(2)]
-        for a in range(2):
-            nc.vector.tensor_copy(v1[a][:], tab_w[a][:].bitcast(U32).indirect(list1[:]))
+        nc.vector.tensor_copy(v1[0][:], tab_w[0][:].bitcast(U32).indirect(list1[:]))
+        for half in range(2):
+            nc.vector.tensor_copy(
+                v1[1][:, half * S // 2 : (half + 1) * S // 2],
+                tab_w[1][:].bitcast(U32).indirect(list1[:, half * S // 32 : (half + 1) * S // 32]))
         for a in range(2):
             nc.vector.tensor_copy(v2[a][:], tab2_w[a][:].bitcast(U32).indirect(list2[:]))
+        nc.vector.tensor_copy(v2_planes[:], tab2_s[:].indirect(list2[:]))
+        seed = [[bank("seed", 4 * b + c) for c in range(NC)] for b in range(2)]
         for b in range(2):
-            accs = [bank("seed", 4 * b + c) for c in range(NC)]
             for c in range(NC):
                 for a in range(2):
                     col = a * H + b * 512
                     nc.tensor.matmul_mx(
-                        out=accs[c][:],
-                        lhsT=v1[a][:, c * JC : (c + 1) * JC].bitcast(FP8X4), lhsT_scale=planes[:, 2 * a * S + c * JC : 2 * a * S + (c + 1) * JC],
-                        rhs=w1_w[:, 2 * col : 2 * (col + 512)].bitcast(FP4X4), rhs_scale=w1_s[:, col : col + 512],
+                        out=seed[b][c][:],
+                        lhsT=v1[a][:, c * JC : (c + 1) * JC].bitcast(FP8X4), lhsT_scale=planes[:, a * S + c * JC : a * S + (c + 1) * JC],
+                        rhs=w1_w[b][:, a, :].bitcast(FP4X4), rhs_scale=w1_s[:, col : col + 512],
                         start=(a == 0), stop=(a == 1))
+        for b in range(2):
             for c in range(NC):
-                nc.scalar.activation(by_t(sig_seed[:, b, c, :]), from_bank(accs[c]), ACT.Sigmoid)
+                nc.scalar.activation(by_t(sig_seed[b][:, c, :]), from_bank(seed[b][c]), ACT.Sigmoid)
+
+        def soil(b, r0, width, pieces, first_bank):
+            share = 512 // width
+            accs = [bank("soil", first_bank + i) for i in range(NC // share)]
+
+            def passes(order):
+                for a, c in order:
+                    codes, scales = pieces[a]
+                    i = c % share
+                    nc.tensor.matmul_mx(
+                        out=accs[c // share][:, i * width : (i + 1) * width],
+                        lhsT=v2[a][:, c * JC : (c + 1) * JC].bitcast(FP8X4), lhsT_scale=v2_planes[4 + 4 * a : P, c * JC : (c + 1) * JC],
+                        rhs=codes.bitcast(FP8X4), rhs_scale=scales, start=(a == 0 and i == 0), stop=(a == 1 and i == share - 1))
+
+            def sigmoids():
+                for i, acc in enumerate(accs):
+                    nc.scalar.activation(
+                        sig_soil[b][:, i * share : (i + 1) * share, :].rearrange("j c (t p) -> j c t p", t=4)[:, :, :, r0 // 4 : (r0 + width) // 4],
+                        acc[:].rearrange("j (c p t) -> j c t p", c=share, t=4), ACT.Sigmoid)
+
+            return passes, sigmoids
+
+        sums = {}
+
+        def turn(c, b, term, unit, start=False, stop=False):
+            for t in range(4):
+                nc.tensor.matmul(
+                    sums[c, b][:, t : 4 * JC : 4], term[:, c, t * P : (t + 1) * P], unit[:],
+                    start=(start and t == 0), stop=(stop and t == 3), is_transpose=True)
+
+        for c in range(NC):
+            sums[c, 0] = bank("sum", c)
+            turn(c, 0, rain[0], ident, start=True)
+        log_seed = sb("log_seed", [P, NC, 512], F32, tag="w1_w1")
+        for c in range(NC):
+            nc.scalar.activation(log_seed[:, c, :], sig_seed[0][:, c, :], ACT.Ln)
 
         passes, sigmoids = soil(0, 0, 512, [columns(quantize_weight("w2_%d" % i, w2_raw[i]), 0, 512) for i in (0, 1)], 4)
-        passes([(a, c) for c in range(NC) for a in range(2)])
+        passes([(a, c) for a in range(2) for c in range(NC)])
+        ident_late = sb("ident_late", [P, P], F32, tag="w2_raw1")
+        nc.vector.tensor_copy(ident_late[:], ident[:])
+        for c in range(NC):
+            turn(c, 0, log_seed, ident_late)
         sigmoids()
         first, low, high = [quantize_weight("w2_%d" % i, w2_raw[i]) for i in (2, 3, 4)]
         parts = [
@@ -201,43 +237,38 @@ def tile_list_seed_bank_germination_kernel(
             passes([(a, c) for a in range(2) for c in range(NC)])
         for passes, sigmoids in parts:
             sigmoids()
-        both = sb("both", [P, NC + 2, 512], F32, tag="w2_4_bf")
+        wo_mx = [quantize_weight("wo_%d" % i, wo_raw[i]) for i in range(2)]
+        both = sb("both", [P, NC - APART, 512], F32)
 
-        def products(b):
-            for c in range(0, NC, 2):
-                nc.vector.tensor_tensor(both[:, c : c + 2, :], sig_seed[:, b, c : c + 2, :], sig_soil[:, b, c : c + 2, :], ALU.mult)
+        def part_of(ap, part):
+            return ap.rearrange("j c (t p) -> j c t p", t=4)[:, :, :, 64 * part : 64 * (part + 1)]
 
-        products(0)
-        nc.vector.tensor_tensor(both[:, NC : NC + 2, :], sig_seed[:, 1, 2:4, :], sig_soil[:, 1, 2:4, :], ALU.mult)
-        wo_mx = [quantize_weight("wo_%d" % b, wo_raw[b]) for b in range(2)]
-
-        logs = sb("logs", [P, 2 * NC + 2, 512], F32, tag="w2_4_q")
-        first_log = [0, 3, 6, 8]
-        sums = {}
-        for b in range(2):
-            for c in range(NC):
-                sums[c, b] = bank("sum", 4 * b + c)
-                for t in range(4):
-                    nc.tensor.matmul(sums[c, b][:, t : 4 * JC : 4], rain[:, c, b, t * P : (t + 1) * P], ident[:], start=(t == 0), stop=False, is_transpose=True)
+        for part in range(2):
+            nc.vector.tensor_tensor(part_of(both[:], part), part_of(sig_seed[1][:, APART:NC, :], part), part_of(sig_soil[1][:, APART:NC, :], part), ALU.mult)
+        wo_mx.append(quantize_weight("wo_2", wo_raw[2]))
         for c in range(NC):
-            nc.scalar.activation(logs[:, first_log[c] + 0, :], both[:, c, :], ACT.Ln)
-            if c < 2:
-                nc.scalar.activation(logs[:, first_log[c] + 1, :], sig_seed[:, 1, c, :], ACT.Ln)
-                nc.scalar.activation(logs[:, first_log[c] + 2, :], sig_soil[:, 1, c, :], ACT.Ln)
+            sums[c, 1] = bank("sum", 4 + c)
+            turn(c, 1, rain[1], ident, start=True)
+
+        late = sb("late", [P, 2 * NC + APART, 512], F32, tag="w2_4_q")
+        logs = [late[:, 0:NC, :], late[:, NC : 2 * NC, :]]
+        log_apart = late[:, 2 * NC : 2 * NC + APART, :]
+        for c in range(NC):
+            nc.scalar.activation(logs[0][:, c, :], sig_soil[0][:, c, :], ACT.Ln)
+            if c < APART:
+                nc.scalar.activation(log_apart[:, c, :], sig_seed[1][:, c, :], ACT.Ln)
+                nc.scalar.activation(logs[1][:, c, :], sig_soil[1][:, c, :], ACT.Ln)
             else:
-                nc.scalar.activation(logs[:, first_log[c] + 1, :], both[:, NC + c - 2, :], ACT.Ln)
+                nc.scalar.activation(logs[1][:, c, :], both[:, c - APART, :], ACT.Ln)
 
         out_v = out.rearrange("(m p) j -> p m j", p=P)
         h_mx = []
         for c in range(NC):
-            h_bf = sb("h_bf%d" % c, [P, 2, JC, 4], BF16, tag="w2_%d_bf" % c)
+            h_bf = sb("h_bf%d" % c, [P, 2, JC, 4], BF16)
             for b in range(2):
-                terms = [(0,), (1, 2) if c < 2 else (1,)][b]
-                for term in terms:
-                    for t in range(4):
-                        nc.tensor.matmul(
-                            sums[c, b][:, t : 4 * JC : 4], logs[:, first_log[c] + term, t * P : (t + 1) * P], ident[:],
-                            start=False, stop=(t == 3 and term == terms[-1]), is_transpose=True)
+                if b == 1 and c < APART:
+                    turn(c, b, log_apart, ident)
+                turn(c, b, logs[b], ident, stop=True)
                 nc.vector.tensor_tensor(
                     h_bf[:, b], sums[c, b][:].rearrange("p (j t) -> p j t", t=4),
                     gain_pt[:, b, :].unsqueeze(1).to_broadcast([P, JC, 4]), ALU.mult)
@@ -254,16 +285,16 @@ def tile_list_seed_bank_germination_kernel(
             groups = [range(4)] if c < NC - 1 else [range(0, 2), range(2, 4)]
             accs = [bank("score", c + g) for g in range(len(groups))]
             for b in range(2):
-                codes, scales = wo_mx[b]
                 for acc, ms in zip(accs, groups):
                     for i, m in enumerate(ms):
+                        codes, scales = columns(wo_mx[m // 2], (m % 2) * P, P) if b == 0 else columns(wo_mx[2], m * P, P)
                         nc.tensor.matmul_mx(
                             out=acc[:, i * JC : (i + 1) * JC],
-                            lhsT=codes[:, m * P : (m + 1) * P].bitcast(FP8X4), lhsT_scale=scales[:, m * P : (m + 1) * P],
+                            lhsT=codes.bitcast(FP8X4), lhsT_scale=scales,
                             rhs=h_q[:, b * JC : (b + 1) * JC].bitcast(FP8X4), rhs_scale=h_s[:, b * JC : (b + 1) * JC],
                             start=(b == 0 and i == 0), stop=(b == 1 and i == len(ms) - 1))
             for g, (acc, ms) in enumerate(zip(accs, groups)):
-                res = sb("res%d%d" % (c, g), [P, len(ms), JC], F32)
+                res = sb("res%d%d" % (c, g), [P, len(ms), JC], F32, tag=["tab_w0", "tab_w1", "tab2_w0", "tab2_w1", "tab3_w"][c + g])
                 flat = res[:].rearrange("p m j -> p (m j)")
                 if g == 0:
                     nc.scalar.copy(flat, acc[:, 0 : len(ms) * JC])

@@ -20,7 +20,8 @@ ALU = mybir.AluOpType
 P = 128
 JC = 128
 NC = S // JC
-APART = 1
+EARLY = 2
+APART = 2
 
 
 def tile_list_seed_bank_germination_kernel(
@@ -70,8 +71,7 @@ def tile_list_seed_bank_germination_kernel(
 
         w2_pieces = [(0, 0, 512), (1, 0, 512), (0, 512, 512), (1, 512, 256), (1, 768, 256)]
         w2_raw = [sb("w2_raw%d" % i, [P, 4, width], F32) for i, (a, c0, width) in enumerate(w2_pieces)]
-        wo_pieces = [(0, 0, 256), (0, 256, 256), (1, 0, 512)]
-        wo_raw = [sb("wo_raw%d" % i, [P, 4, width], F32) for i, (b, n0, width) in enumerate(wo_pieces)]
+        wo_raw = [sb("wo_raw%d" % b, [P, 4, N], F32) for b in range(2)]
 
         def load_w2(i):
             a, c0, width = w2_pieces[i]
@@ -117,8 +117,8 @@ def tile_list_seed_bank_germination_kernel(
         for i in range(len(w2_pieces)):
             load_w2(i)
         nc.sync.dma_start(out=gain_pt[:], in_=gain.rearrange("(b p t) -> p b t", b=2, t=4))
-        for i, (b, n0, width) in enumerate(wo_pieces):
-            nc.sync.dma_start(out=wo_raw[i][:], in_=wo[512 * b : 512 * (b + 1), n0 : n0 + width].rearrange("(p t) n -> p t n", t=4))
+        for b in range(2):
+            nc.sync.dma_start(out=wo_raw[b][:], in_=wo[512 * b : 512 * (b + 1), :].rearrange("(p t) n -> p t n", t=4))
 
         make_identity(nc, ident[:])
 
@@ -215,29 +215,36 @@ def tile_list_seed_bank_germination_kernel(
                     sums[c, b][:, t : 4 * JC : 4], term[:, c, t * P : (t + 1) * P], unit[:],
                     start=(start and t == 0), stop=(stop and t == 3), is_transpose=True)
 
-        for c in range(NC):
+        for c in range(EARLY):
             sums[c, 0] = bank("sum", c)
             turn(c, 0, rain[0], ident, start=True)
-        log_seed = sb("log_seed", [P, NC, 512], F32, tag="w1_w1")
-        for c in range(NC):
+        log_seed = sb("log_seed", [P, EARLY, 512], F32, tag="w1_w1")
+        for c in range(EARLY):
             nc.scalar.activation(log_seed[:, c, :], sig_seed[0][:, c, :], ACT.Ln)
 
         passes, sigmoids = soil(0, 0, 512, [columns(quantize_weight("w2_%d" % i, w2_raw[i]), 0, 512) for i in (0, 1)], 4)
         passes([(a, c) for a in range(2) for c in range(NC)])
         ident_late = sb("ident_late", [P, P], F32, tag="w2_raw1")
         nc.vector.tensor_copy(ident_late[:], ident[:])
-        for c in range(NC):
+        for c in range(EARLY):
             turn(c, 0, log_seed, ident_late)
         sigmoids()
         first, low, high = [quantize_weight("w2_%d" % i, w2_raw[i]) for i in (2, 3, 4)]
         parts = [
-            soil(1, 0, 256, [columns(first, 0, 256), columns(low, 0, 256)], 4),
-            soil(1, 256, 256, [columns(first, 256, 256), columns(high, 0, 256)], 6)]
+            soil(1, 0, 256, [columns(first, 0, 256), columns(low, 0, 256)], 2),
+            soil(1, 256, 256, [columns(first, 256, 256), columns(high, 0, 256)], 4)]
         for passes, sigmoids in parts:
             passes([(a, c) for a in range(2) for c in range(NC)])
         for passes, sigmoids in parts:
             sigmoids()
-        wo_mx = [quantize_weight("wo_%d" % i, wo_raw[i]) for i in range(2)]
+        ident_last = sb("ident_last", [P, P], F32, tag="w2_raw4")
+        nc.vector.tensor_copy(ident_last[:], ident[:])
+        for c in range(EARLY, NC):
+            sums[c, 0] = bank("sum", 4 + c)
+            turn(c, 0, rain[0], ident_last, start=True)
+        both0 = sb("both0", [P, NC - EARLY, 512], F32, tag="w2_4_bf")
+        nc.vector.tensor_tensor(both0[:], sig_seed[0][:, EARLY:NC, :], sig_soil[0][:, EARLY:NC, :], ALU.mult)
+        wo_mx = [quantize_weight("wo_0", wo_raw[0])]
         both = sb("both", [P, NC - APART, 512], F32)
 
         def part_of(ap, part):
@@ -245,16 +252,16 @@ def tile_list_seed_bank_germination_kernel(
 
         for part in range(2):
             nc.vector.tensor_tensor(part_of(both[:], part), part_of(sig_seed[1][:, APART:NC, :], part), part_of(sig_soil[1][:, APART:NC, :], part), ALU.mult)
-        wo_mx.append(quantize_weight("wo_2", wo_raw[2]))
+        wo_mx.append(quantize_weight("wo_1", wo_raw[1]))
         for c in range(NC):
-            sums[c, 1] = bank("sum", 4 + c)
-            turn(c, 1, rain[1], ident, start=True)
+            sums[c, 1] = bank("sum", 2 + c)
+            turn(c, 1, rain[1], ident_last, start=True)
 
         late = sb("late", [P, 2 * NC + APART, 512], F32, tag="w2_4_q")
         logs = [late[:, 0:NC, :], late[:, NC : 2 * NC, :]]
         log_apart = late[:, 2 * NC : 2 * NC + APART, :]
         for c in range(NC):
-            nc.scalar.activation(logs[0][:, c, :], sig_soil[0][:, c, :], ACT.Ln)
+            nc.scalar.activation(logs[0][:, c, :], sig_soil[0][:, c, :] if c < EARLY else both0[:, c - EARLY, :], ACT.Ln)
             if c < APART:
                 nc.scalar.activation(log_apart[:, c, :], sig_seed[1][:, c, :], ACT.Ln)
                 nc.scalar.activation(logs[1][:, c, :], sig_soil[1][:, c, :], ACT.Ln)
@@ -283,11 +290,11 @@ def tile_list_seed_bank_germination_kernel(
         for c in range(NC):
             h_q, h_s = h_mx[c]
             groups = [range(4)] if c < NC - 1 else [range(0, 2), range(2, 4)]
-            accs = [bank("score", c + g) for g in range(len(groups))]
+            accs = [bank("score", [0, 1, 6, 7, 2][c + g]) for g in range(len(groups))]
             for b in range(2):
                 for acc, ms in zip(accs, groups):
                     for i, m in enumerate(ms):
-                        codes, scales = columns(wo_mx[m // 2], (m % 2) * P, P) if b == 0 else columns(wo_mx[2], m * P, P)
+                        codes, scales = columns(wo_mx[b], m * P, P)
                         nc.tensor.matmul_mx(
                             out=acc[:, i * JC : (i + 1) * JC],
                             lhsT=codes.bitcast(FP8X4), lhsT_scale=scales,

@@ -53,17 +53,16 @@ def tile_list_seed_bank_germination_kernel(
         w1_s = sb("w1_s", [P, 2 * H], U8)
         w3_w = sb("w3_w", [P, H], I32)
         w3_s = sb("w3_s", [P, H], U8)
-        planes = sb("planes", [P, 2 * S], U8)
-        v2_planes = sb("v2_planes", [P, S], U8)
+        planes = sb("planes", [P, 4 * S], U8)
         v3_plane = sb("v3_plane", [P, S], U8)
         gain_pt = sb("gain_pt", [P, 2, 4], F32)
         ident = sb("ident", [P, P], F32)
 
         nc.vector.memset(tab3_s[:].bitcast(I32), 0)
         nc.vector.memset(tab_s[:].bitcast(I32), 0)
+        nc.vector.memset(tab2_s[:].bitcast(I32), 0)
         nc.vector.memset(w1_s[:].bitcast(I32), 0)
         nc.vector.memset(planes[:].bitcast(I32), 0)
-        nc.vector.memset(tab2_s[:].bitcast(I32), 0)
         warm = sb("warm", [P, 2], F32)
         nc.gpsimd.memset(warm[:, 0:1], 0.0)
         nc.scalar.activation(warm[:, 1:2], warm[:, 0:1], ACT.Sigmoid)
@@ -92,6 +91,8 @@ def tile_list_seed_bank_germination_kernel(
         load_words(w3_w, w3_words[0])
         nc.sync.dma_start(list1[:], offs)
         nc.sync.dma_start(out=tab_s[0:P:4, :].bitcast(I32), in_=tab_scales.rearrange("a q t -> q a t").bitcast(I32))
+        nc.sync.dma_start(list2[:], offs2)
+        nc.sync.dma_start(out=tab2_s[0:P:4, :].bitcast(I32), in_=tab2_scales.rearrange("a q t -> q a t").bitcast(I32))
         load_words(tab_w[0], tab_words[0])
         for q in range(4):
             nc.sync.dma_start(
@@ -100,20 +101,18 @@ def tile_list_seed_bank_germination_kernel(
         load_w1(0)
         load_words(tab_w[1], tab_words[1])
         v3 = sb("v3", [P, S], U16)
-        rows = sb("rows", [P, S], U8)
+        rows = sb("rows", [P, 2 * S], U8)
         nc.vector.tensor_copy(v3[:], tab3_w[:].indirect(list3[:]))
         nc.vector.tensor_copy(v3_plane[:], tab3_s[:].indirect(list3[:]))
-        nc.vector.tensor_copy(rows[:], tab_s[:].indirect(list1[:]))
+        nc.vector.tensor_copy(rows[:, 0:S], tab_s[:].indirect(list1[:]))
+        nc.vector.tensor_copy(rows[:, S : 2 * S], tab2_s[:].indirect(list2[:]))
         for q in (0, 2, 1, 3):
             nc.sync.dma_start(
                 out=planes[32 * q : 32 * q + 4, :].rearrange("p (a j) -> p a j", a=2).bitcast(I32),
                 in_=rows[32 * q : 32 * q + 32 : 4, :].bitcast(I32))
-        nc.sync.dma_start(list2[:], offs2)
         load_w1(1)
         for a in range(2):
             load_words(tab2_w[a], tab2_words[a])
-        for q in range(4):
-            nc.sync.dma_start(out=tab2_s[32 * q + 4 : 32 * q + 12, :].bitcast(I32), in_=tab2_scales[:, 4 * q : 4 * q + 4, :].bitcast(I32))
         for i in range(len(w2_pieces)):
             load_w2(i)
         nc.sync.dma_start(out=gain_pt[:], in_=gain.rearrange("(b p t) -> p b t", b=2, t=4))
@@ -171,7 +170,6 @@ def tile_list_seed_bank_germination_kernel(
                 tab_w[1][:].bitcast(U32).indirect(list1[:, half * S // 32 : (half + 1) * S // 32]))
         for a in range(2):
             nc.vector.tensor_copy(v2[a][:], tab2_w[a][:].bitcast(U32).indirect(list2[:]))
-        nc.vector.tensor_copy(v2_planes[:], tab2_s[:].indirect(list2[:]))
         seed = [[bank("seed", 4 * b + c) for c in range(NC)] for b in range(2)]
         for b in range(2):
             for c in range(NC):
@@ -179,7 +177,7 @@ def tile_list_seed_bank_germination_kernel(
                     col = a * H + b * 512
                     nc.tensor.matmul_mx(
                         out=seed[b][c][:],
-                        lhsT=v1[a][:, c * JC : (c + 1) * JC].bitcast(FP8X4), lhsT_scale=planes[:, a * S + c * JC : a * S + (c + 1) * JC],
+                        lhsT=v1[a][:, c * JC : (c + 1) * JC].bitcast(FP8X4), lhsT_scale=planes[:, 2 * a * S + c * JC : 2 * a * S + (c + 1) * JC],
                         rhs=w1_w[b][:, a, :].bitcast(FP4X4), rhs_scale=w1_s[:, col : col + 512],
                         start=(a == 0), stop=(a == 1))
         for b in range(2):
@@ -196,7 +194,7 @@ def tile_list_seed_bank_germination_kernel(
                     i = c % share
                     nc.tensor.matmul_mx(
                         out=accs[c // share][:, i * width : (i + 1) * width],
-                        lhsT=v2[a][:, c * JC : (c + 1) * JC].bitcast(FP8X4), lhsT_scale=v2_planes[4 + 4 * a : P, c * JC : (c + 1) * JC],
+                        lhsT=v2[a][:, c * JC : (c + 1) * JC].bitcast(FP8X4), lhsT_scale=planes[:, (2 * a + 1) * S + c * JC : (2 * a + 1) * S + (c + 1) * JC],
                         rhs=codes.bitcast(FP8X4), rhs_scale=scales, start=(a == 0 and i == 0), stop=(a == 1 and i == share - 1))
 
             def sigmoids():

from contextlib import ExitStack

import concourse.mybir as mybir
from concourse.masks import make_identity

K1, K2, K3, H, N, T1, T2, T3, S = 1024, 1024, 512, 1024, 512, 2048, 1024, 2048, 512
FLOPS = 2 * S * (K1 * H + K2 * H + K3 * H + H * N)

F32 = mybir.dt.float32
BF16 = mybir.dt.bfloat16
I32 = mybir.dt.int32
U32 = mybir.dt.uint32
U16 = mybir.dt.uint16
U8 = mybir.dt.uint8
FP8X4 = mybir.dt.float8_e4m3fn_x4
FP4X4 = mybir.dt.float4_e2m1fn_x4
ACT = mybir.ActivationFunctionType
ALU = mybir.AluOpType

P = 128
JC = 128
NC = S // JC
EARLY = 2
APART = 2


def tile_list_seed_bank_germination_kernel(
    tc, tab_words, tab_scales, tab2_words, tab2_scales, tab3_words, tab3_scales, offs, offs2, offs3,
    w1_words, w1_scales, w2, w3_words, w3_scales, gain, wo, out,
):
    nc = tc.nc
    with ExitStack() as ctx:
        keep = ctx.enter_context(tc.tile_pool(name="keep", bufs=1))
        psum = ctx.enter_context(tc.psum_pool(name="psum", bufs=1))

        def sb(name, shape, dtype, tag=None):
            return keep.tile(shape, dtype, name=name, tag=tag or name, align_bytes=64)

        def bank(name, number):
            return psum.tile([P, 512], F32, name=name, tag="bank%d" % number)

        list1 = keep.tile([P, S // 16], U16, name="list1")
        list2 = keep.tile([P, S // 16], U16, name="list2")
        list3 = keep.tile([P, S // 16], U16, name="list3")

        tab_w = [sb("tab_w%d" % a, [P, T1], I32) for a in range(2)]
        tab_s = sb("tab_s", [P, T1], U8)
        tab2_w = [sb("tab2_w%d" % a, [P, T2], I32) for a in range(2)]
        tab2_s = sb("tab2_s", [P, T2], U8)
        tab3_w = sb("tab3_w", [P, T3], U16)
        tab3_s = sb("tab3_s", [P, T3], U8)
        w1_w = [sb("w1_w%d" % b, [P, 2, H], U8) for b in range(2)]
        w1_s = sb("w1_s", [P, 2 * H], U8)
        w3_w = sb("w3_w", [P, H], I32)
        w3_s = sb("w3_s", [P, H], U8)
        planes = sb("planes", [P, 4 * S], U8)
        v3_plane = sb("v3_plane", [P, S], U8)
        gain_pt = sb("gain_pt", [P, 2, 4], F32)
        ident = sb("ident", [P, P], F32)

        nc.vector.memset(tab3_s[:].bitcast(I32), 0)
        nc.vector.memset(tab_s[:].bitcast(I32), 0)
        nc.vector.memset(tab2_s[:].bitcast(I32), 0)
        nc.vector.memset(w1_s[:].bitcast(I32), 0)
        nc.vector.memset(planes[:].bitcast(I32), 0)
        warm = sb("warm", [P, 2], F32)
        nc.gpsimd.memset(warm[:, 0:1], 0.0)
        nc.scalar.activation(warm[:, 1:2], warm[:, 0:1], ACT.Sigmoid)
        nc.gpsimd.memset(w3_s[:].bitcast(I32), 0)

        w2_pieces = [(0, 0, 512), (1, 0, 512), (0, 512, 512), (1, 512, 256), (1, 768, 256)]
        w2_raw = [sb("w2_raw%d" % i, [P, 4, width], F32) for i, (a, c0, width) in enumerate(w2_pieces)]
        wo_raw = [sb("wo_raw%d" % b, [P, 4, N], F32) for b in range(2)]

        def load_w2(i):
            a, c0, width = w2_pieces[i]
            nc.sync.dma_start(out=w2_raw[i][:], in_=w2[512 * a : 512 * (a + 1), c0 : c0 + width].rearrange("(p j) c -> p j c", j=4))

        def load_words(tile, words):
            nc.sync.dma_start(out=tile[:], in_=words.rearrange("p t i -> p (t i)").bitcast(I32))

        def load_w1(b):
            nc.sync.dma_start(out=w1_w[b][:].bitcast(I32), in_=w1_words[:, :, b * H : (b + 1) * H].rearrange("a p c -> p a c").bitcast(I32))

        for q in range(4):
            nc.gpsimd.dma_start(out=w3_s[q:P:32, :].bitcast(I32), in_=w3_scales[0, q:16:4, :].bitcast(I32))
        nc.sync.dma_start(list3[:], offs3)
        nc.sync.dma_start(out=tab3_w[:].bitcast(I32), in_=tab3_words[0].bitcast(I32))
        for q in range(4):
            nc.sync.dma_start(out=tab3_s[q:P:32, :].bitcast(I32), in_=tab3_scales[0, q:16:4, :].bitcast(I32))
        load_words(w3_w, w3_words[0])
        nc.sync.dma_start(list1[:], offs)
        nc.sync.dma_start(out=tab_s[0:P:4, :].bitcast(I32), in_=tab_scales.rearrange("a q t -> q a t").bitcast(I32))
        nc.sync.dma_start(list2[:], offs2)
        nc.sync.dma_start(out=tab2_s[0:P:4, :].bitcast(I32), in_=tab2_scales.rearrange("a q t -> q a t").bitcast(I32))
        load_words(tab_w[0], tab_words[0])
        for q in range(4):
            nc.sync.dma_start(
                out=w1_s[q:P:32, :].rearrange("p (a c) -> p a c", a=2).bitcast(I32),
                in_=w1_scales[:, q:16:4, :].rearrange("a r c -> r a c").bitcast(I32))
        load_w1(0)
        load_words(tab_w[1], tab_words[1])
        v3 = sb("v3", [P, S], U16)
        rows = sb("rows", [P, 2 * S], U8)
        nc.vector.tensor_copy(v3[:], tab3_w[:].indirect(list3[:]))
        nc.vector.tensor_copy(v3_plane[:], tab3_s[:].indirect(list3[:]))
        nc.vector.tensor_copy(rows[:, 0:S], tab_s[:].indirect(list1[:]))
        nc.vector.tensor_copy(rows[:, S : 2 * S], tab2_s[:].indirect(list2[:]))
        for q in (0, 2, 1, 3):
            nc.sync.dma_start(
                out=planes[32 * q : 32 * q + 4, :].rearrange("p (a j) -> p a j", a=2).bitcast(I32),
                in_=rows[32 * q : 32 * q + 32 : 4, :].bitcast(I32))
        load_w1(1)
        for a in range(2):
            load_words(tab2_w[a], tab2_words[a])
        for i in range(len(w2_pieces)):
            load_w2(i)
        nc.sync.dma_start(out=gain_pt[:], in_=gain.rearrange("(b p t) -> p b t", b=2, t=4))
        for b in range(2):
            nc.sync.dma_start(out=wo_raw[b][:], in_=wo[512 * b : 512 * (b + 1), :].rearrange("(p t) n -> p t n", t=4))

        make_identity(nc, ident[:])

        def round_weight(name, raw):
            grouped = sb(name + "_bf", [P, 4 * raw.shape[2]], BF16)
            dst = grouped[:].rearrange("p (x w t) -> p x t w", w=4, t=4)
            src = raw[:].rearrange("p t (x w) -> p x t w", w=4)
            nc.vector.tensor_copy(dst, src)
            return grouped

        def quantize(name, grouped):
            width = grouped.shape[1] // 4
            codes = sb(name + "_q", [P, width], U32)
            scales = sb(name + "_s", [P, width], U8)
            nc.vector.quantize_mx(out=codes[:].bitcast(FP8X4), scales=scales[:], in_=grouped[:])
            return codes, scales

        def quantize_weight(name, raw):
            return quantize(name, round_weight(name, raw))

        def columns(mx, c0, width):
            return mx[0][:, c0 : c0 + width], mx[1][:, c0 : c0 + width]

        def by_t(ap):
            return ap.rearrange("j (t p) -> j t p", t=4)

        def from_bank(acc):
            return acc[:].rearrange("j (p t) -> j t p", t=4)

        sig_seed = [sb("sig_seed%d" % b, [P, NC, 512], F32) for b in range(2)]
        sig_soil = [sb("sig_soil%d" % b, [P, NC, 512], F32) for b in range(2)]
        rain = [sb("rain%d" % b, [P, NC, 512], F32) for b in range(2)]

        for c in range(NC):
            for b in range(2):
                acc = bank("rain", 2 * c + b)
                nc.tensor.matmul_mx(
                    out=acc[:],
                    lhsT=v3[:, c * JC : (c + 1) * JC].bitcast(FP4X4), lhsT_scale=v3_plane[:, c * JC : (c + 1) * JC],
                    rhs=w3_w[:, b * 512 : (b + 1) * 512].bitcast(FP8X4), rhs_scale=w3_s[:, b * 512 : (b + 1) * 512],
                    start=True, stop=True)
                nc.scalar.copy(by_t(rain[b][:, c, :]), from_bank(acc))

        v1 = [sb("v1_%d" % a, [P, S], U32) for a in range(2)]
        v2 = [sb("v2_%d" % a, [P, S], U32) for a in range(2)]
        nc.vector.tensor_copy(v1[0][:], tab_w[0][:].bitcast(U32).indirect(list1[:]))
        for half in range(2):
            nc.vector.tensor_copy(
                v1[1][:, half * S // 2 : (half + 1) * S // 2],
                tab_w[1][:].bitcast(U32).indirect(list1[:, half * S // 32 : (half + 1) * S // 32]))
        for a in range(2):
            nc.vector.tensor_copy(v2[a][:], tab2_w[a][:].bitcast(U32).indirect(list2[:]))
        seed = [[bank("seed", 4 * b + c) for c in range(NC)] for b in range(2)]
        for b in range(2):
            for c in range(NC):
                for a in range(2):
                    col = a * H + b * 512
                    nc.tensor.matmul_mx(
                        out=seed[b][c][:],
                        lhsT=v1[a][:, c * JC : (c + 1) * JC].bitcast(FP8X4), lhsT_scale=planes[:, 2 * a * S + c * JC : 2 * a * S + (c + 1) * JC],
                        rhs=w1_w[b][:, a, :].bitcast(FP4X4), rhs_scale=w1_s[:, col : col + 512],
                        start=(a == 0), stop=(a == 1))
        for b in range(2):
            for c in range(NC):
                nc.scalar.activation(by_t(sig_seed[b][:, c, :]), from_bank(seed[b][c]), ACT.Sigmoid)

        def soil(b, r0, width, pieces, first_bank):
            share = 512 // width
            accs = [bank("soil", first_bank + i) for i in range(NC // share)]

            def passes(order):
                for a, c in order:
                    codes, scales = pieces[a]
                    i = c % share
                    nc.tensor.matmul_mx(
                        out=accs[c // share][:, i * width : (i + 1) * width],
                        lhsT=v2[a][:, c * JC : (c + 1) * JC].bitcast(FP8X4), lhsT_scale=planes[:, (2 * a + 1) * S + c * JC : (2 * a + 1) * S + (c + 1) * JC],
                        rhs=codes.bitcast(FP8X4), rhs_scale=scales, start=(a == 0 and i == 0), stop=(a == 1 and i == share - 1))

            def sigmoids():
                for i, acc in enumerate(accs):
                    nc.scalar.activation(
                        sig_soil[b][:, i * share : (i + 1) * share, :].rearrange("j c (t p) -> j c t p", t=4)[:, :, :, r0 // 4 : (r0 + width) // 4],
                        acc[:].rearrange("j (c p t) -> j c t p", c=share, t=4), ACT.Sigmoid)

            return passes, sigmoids

        sums = {}

        def turn(c, b, term, unit, start=False, stop=False):
            for t in range(4):
                nc.tensor.matmul(
                    sums[c, b][:, t : 4 * JC : 4], term[:, c, t * P : (t + 1) * P], unit[:],
                    start=(start and t == 0), stop=(stop and t == 3), is_transpose=True)

        for c in range(EARLY):
            sums[c, 0] = bank("sum", c)
            turn(c, 0, rain[0], ident, start=True)
        log_seed = sb("log_seed", [P, EARLY, 512], F32, tag="w1_w1")
        for c in range(EARLY):
            nc.scalar.activation(log_seed[:, c, :], sig_seed[0][:, c, :], ACT.Ln)

        passes, sigmoids = soil(0, 0, 512, [columns(quantize_weight("w2_%d" % i, w2_raw[i]), 0, 512) for i in (0, 1)], 4)
        passes([(a, c) for a in range(2) for c in range(NC)])
        ident_late = sb("ident_late", [P, P], F32, tag="w2_raw1")
        nc.vector.tensor_copy(ident_late[:], ident[:])
        for c in range(EARLY):
            turn(c, 0, log_seed, ident_late)
        sigmoids()
        first, low, high = [quantize_weight("w2_%d" % i, w2_raw[i]) for i in (2, 3, 4)]
        parts = [
            soil(1, 0, 256, [columns(first, 0, 256), columns(low, 0, 256)], 2),
            soil(1, 256, 256, [columns(first, 256, 256), columns(high, 0, 256)], 4)]
        for passes, sigmoids in parts:
            passes([(a, c) for a in range(2) for c in range(NC)])
        for passes, sigmoids in parts:
            sigmoids()
        ident_last = sb("ident_last", [P, P], F32, tag="w2_raw4")
        nc.vector.tensor_copy(ident_last[:], ident[:])
        for c in range(EARLY, NC):
            sums[c, 0] = bank("sum", 4 + c)
            turn(c, 0, rain[0], ident_last, start=True)
        both0 = sb("both0", [P, NC - EARLY, 512], F32, tag="w2_4_bf")
        nc.vector.tensor_tensor(both0[:], sig_seed[0][:, EARLY:NC, :], sig_soil[0][:, EARLY:NC, :], ALU.mult)
        wo_mx = [quantize_weight("wo_0", wo_raw[0])]
        both = sb("both", [P, NC - APART, 512], F32)

        def part_of(ap, part):
            return ap.rearrange("j c (t p) -> j c t p", t=4)[:, :, :, 64 * part : 64 * (part + 1)]

        for part in range(2):
            nc.vector.tensor_tensor(part_of(both[:], part), part_of(sig_seed[1][:, APART:NC, :], part), part_of(sig_soil[1][:, APART:NC, :], part), ALU.mult)
        wo_mx.append(quantize_weight("wo_1", wo_raw[1]))
        for c in range(NC):
            sums[c, 1] = bank("sum", 2 + c)
            turn(c, 1, rain[1], ident_last, start=True)

        late = sb("late", [P, 2 * NC + APART, 512], F32, tag="w2_4_q")
        logs = [late[:, 0:NC, :], late[:, NC : 2 * NC, :]]
        log_apart = late[:, 2 * NC : 2 * NC + APART, :]
        for c in range(NC):
            nc.scalar.activation(logs[0][:, c, :], sig_soil[0][:, c, :] if c < EARLY else both0[:, c - EARLY, :], ACT.Ln)
            if c < APART:
                nc.scalar.activation(log_apart[:, c, :], sig_seed[1][:, c, :], ACT.Ln)
                nc.scalar.activation(logs[1][:, c, :], sig_soil[1][:, c, :], ACT.Ln)
            else:
                nc.scalar.activation(logs[1][:, c, :], both[:, c - APART, :], ACT.Ln)

        out_v = out.rearrange("(m p) j -> p m j", p=P)
        h_mx = []
        for c in range(NC):
            h_bf = sb("h_bf%d" % c, [P, 2, JC, 4], BF16)
            for b in range(2):
                if b == 1 and c < APART:
                    turn(c, b, log_apart, ident)
                turn(c, b, logs[b], ident, stop=True)
                nc.vector.tensor_tensor(
                    h_bf[:, b], sums[c, b][:].rearrange("p (j t) -> p j t", t=4),
                    gain_pt[:, b, :].unsqueeze(1).to_broadcast([P, JC, 4]), ALU.mult)
            h_q = sb("h_q%d" % c, [P, 2 * JC], U32)
            h_s = sb("h_s%d" % c, [P, 2 * JC], U8)
            for b0, b1 in ([(0, 2)] if c < NC - 1 else [(0, 1), (1, 2)]):
                nc.vector.quantize_mx(
                    out=h_q[:, b0 * JC : b1 * JC].bitcast(FP8X4), scales=h_s[:, b0 * JC : b1 * JC],
                    in_=h_bf[:, b0:b1].rearrange("p b j t -> p (b j t)"))
            h_mx.append((h_q, h_s))

        for c in range(NC):
            h_q, h_s = h_mx[c]
            groups = [range(4)] if c < NC - 1 else [range(0, 2), range(2, 4)]
            accs = [bank("score", [0, 1, 6, 7, 2][c + g]) for g in range(len(groups))]
            for b in range(2):
                for acc, ms in zip(accs, groups):
                    for i, m in enumerate(ms):
                        codes, scales = columns(wo_mx[b], m * P, P)
                        nc.tensor.matmul_mx(
                            out=acc[:, i * JC : (i + 1) * JC],
                            lhsT=codes.bitcast(FP8X4), lhsT_scale=scales,
                            rhs=h_q[:, b * JC : (b + 1) * JC].bitcast(FP8X4), rhs_scale=h_s[:, b * JC : (b + 1) * JC],
                            start=(b == 0 and i == 0), stop=(b == 1 and i == len(ms) - 1))
            for g, (acc, ms) in enumerate(zip(accs, groups)):
                res = sb("res%d%d" % (c, g), [P, len(ms), JC], F32, tag=["tab_w0", "tab_w1", "tab2_w0", "tab2_w1", "tab3_w"][c + g])
                flat = res[:].rearrange("p m j -> p (m j)")
                if g == 0:
                    nc.scalar.copy(flat, acc[:, 0 : len(ms) * JC])
                else:
                    nc.vector.tensor_copy(flat, acc[:, 0 : len(ms) * JC])
                nc.sync.dma_start(out=out_v[:, ms.start : ms.stop, c * JC : (c + 1) * JC], in_=res[:])
